import numpy as np
import ml_dtypes


def mxq(x, axis, fmt="e4m3"):
    dtype, down = {"e4m3": (ml_dtypes.float8_e4m3fn, 7), "e5m2": (ml_dtypes.float8_e5m2, 14)}[fmt]
    v = np.moveaxis(np.asarray(x, np.float32).astype(ml_dtypes.bfloat16).astype(np.float64), axis, -1)
    blocks = v.reshape(v.shape[:-1] + (-1, 32))
    amax = np.abs(blocks).max(-1, keepdims=True)
    byte = np.maximum(np.where(amax > 0, np.frexp(amax)[1] - 1 + 127, 0) - down, 1)
    scale = np.exp2(byte - 127.0)
    codes = (blocks / scale).astype(np.float32).astype(dtype).astype(np.float64)
    return np.moveaxis((codes * scale).reshape(v.shape), -1, axis)


WIDE = False


def mx_kscale(k):
    if not WIDE:
        return np.ones(k)
    levels = np.array([18, -18])
    if k % 512:
        return np.exp2(np.random.permutation(np.resize(levels, k // 32))).repeat(32)
    a = np.empty((k // 512, 16))
    for p in range(k // 512):
        a[p, :8] = np.random.permutation(np.resize(levels, 8))
        for g in range(8):
            far = levels[np.abs(levels - a[p, g]) >= 10]
            a[p, g + 8] = far[np.random.randint(len(far))]
    return np.exp2(a.ravel()).repeat(32)


def f64(x):
    return np.asarray(x).astype(np.float64)


def striped(idx):
    return np.tile(np.asarray(idx).reshape(-1, 16).T, (8, 1)).astype(np.uint16)


def unstriped(offs):
    return offs[:16].T.reshape(-1).astype(np.int64)


def eight(idx):
    return np.concatenate([idx[h].reshape(-1, 16).T for h in range(8)]).astype(np.uint16)


def uneight(offs):
    return np.stack([offs[16 * h:16 * h + 16].T.reshape(-1) for h in range(8)]).astype(np.int64)

def planes(y):
    n, m = y.shape
    v = y.astype(np.float32).astype(ml_dtypes.bfloat16).astype(np.float64).reshape(n // 32, 32, m)
    top = np.abs(v).max(1)
    byte = np.clip(np.where(top > 0, np.frexp(top)[1] - 1 + 127 - 7, 1), 1, 254)
    codes = (v * np.exp2(127.0 - byte)[:, None, :]).reshape(n, m).astype(np.float32).astype(ml_dtypes.float8_e4m3fn).view(np.uint8)
    words = codes.reshape(n // 512, 128, 4, m).transpose(0, 1, 3, 2)
    return np.ascontiguousarray(words), np.ascontiguousarray(byte.astype(np.uint8).reshape(n // 512, 16, m))


def setup_inputs():
    n = np.random.standard_normal
    uni = np.random.uniform
    place = np.stack([np.random.permutation(512) for _ in range(8)])
    f_d = mx_kscale(512)
    f_e = mx_kscale(512)
    return {
        "wo": (n((512, 512)) / np.sqrt(512) * f_e[:, None] * f_d[None, :]).astype(np.float32),
        "dyT": (n((512, 512)) / f_e[:, None]).astype(np.float32),
        "W": (n((512, 512)) / np.sqrt(512) / f_d[:, None]).astype(np.float32),
        "h": (np.tanh(2.0 * n((512, 512)))).astype(np.float32),
        "offs": eight(place),
    }


def reference(wo, dyT, W, h, offs):
    place = uneight(offs)
    u = mxq(f64(wo), 0, "e4m3").T @ mxq(f64(dyT), 0, "e5m2")
    ui = np.concatenate([u[64 * run:64 * run + 64][:, place[run % 8]] for run in range(8)])
    dz = ui * (1.0 - np.square(f64(h)))
    out_0 = mxq(f64(W), 0, "e4m3").T @ mxq(dz, 0, "e5m2")
    return (out_0,) + planes(out_0)

@@ -1,0 +1,183 @@
+from contextlib import ExitStack
+
+import concourse.mybir as mybir
+
+F32 = mybir.dt.float32
+BF16 = mybir.dt.bfloat16
+I32 = mybir.dt.int32
+U32 = mybir.dt.uint32
+U16 = mybir.dt.uint16
+U8 = mybir.dt.uint8
+E4M3 = mybir.dt.float8_e4m3fn_x4
+E5M2 = mybir.dt.float8_e5m2_x4
+ALU = mybir.AluOpType
+ACT = mybir.ActivationFunctionType
+
+P = 128
+PACK = 4
+N = 512
+HALF = N // 2
+FLOPS = 2 * 2 * N * N * N
+
+
+def quantise(nc, codes, scales, grouped, fmt, c0, c1):
+    nc.vector.quantize_mx(
+        out=codes[:, c0:c1].bitcast(fmt),
+        scales=scales[:, c0:c1],
+        in_=grouped[:, c0 * PACK : c1 * PACK],
+    )
+
+
+def tile_attend_ghsort_tnh_pl_kernel(tc, wo, dyT, W, h, offs, out_0, out_1, out_2):
+    nc = tc.nc
+    with ExitStack() as ctx:
+        sb = ctx.enter_context(tc.tile_pool(name="sb", bufs=1))
+        ps = ctx.enter_context(tc.psum_pool(name="ps", bufs=1))
+
+        offsets = sb.tile([P, N // 16], U16, name="offsets")
+        wo_raw = [sb.tile([P, PACK, HALF], F32, name="wo_raw%d" % a) for a in range(2)]
+        dy_raw = sb.tile([P, PACK, N], F32, name="dy_raw")
+        h_raw = sb.tile([P, PACK, N], F32, name="h_raw")
+        w_raw = sb.tile([P, PACK, N], F32, name="w_raw")
+
+        nc.sync.dma_start(out=dy_raw[:], in_=dyT.rearrange("(p j) c -> p j c", j=PACK))
+        wo_rows = wo.rearrange("(p j) c -> p j c", j=PACK)
+        for a in range(2):
+            nc.sync.dma_start(out=wo_raw[a][:], in_=wo_rows[:, :, a * HALF : (a + 1) * HALF])
+        nc.sync.dma_start(offsets[:], offs)
+        nc.sync.dma_start(out=h_raw[:], in_=h.rearrange("(p j) c -> p j c", j=PACK))
+        nc.sync.dma_start(out=w_raw[:], in_=W.rearrange("(p j) c -> p j c", j=PACK))
+
+        def operand(name):
+            grouped = sb.tile([P, N * PACK], BF16, name=name + "_bf", align_bytes=64)
+            codes = sb.tile([P, N], U32, name=name + "_codes", align_bytes=64)
+            scales = sb.tile([P, N], U8, name=name + "_scales", align_bytes=64)
+            return grouped, codes, scales
+
+        wo_bf, wo_codes, wo_scales = operand("wo")
+        wo_hi = sb.tile([P, N * PACK], BF16, name="wo_hi", align_bytes=64)
+        dy_bf, dy_codes, dy_scales = operand("dy")
+        w_bf, w_codes, w_scales = operand("w")
+        dz_bf, dz_codes, dz_scales = operand("dz")
+        y_bf, y_codes, y_scales = operand("y")
+
+        def weave(tile, c0, c1):
+            return tile[:, c0 * PACK : c1 * PACK].rearrange("p (c i j) -> p c j i", i=4, j=PACK)
+
+        def runs(raw, c0, c1):
+            return raw[:, :, c0:c1].rearrange("p j (c i) -> p c j i", i=4)
+
+        cut = 320
+        nc.vector.tensor_copy(out=weave(dy_bf, 0, cut), in_=runs(dy_raw, 0, cut))
+        nc.scalar.activation(out=weave(dy_bf, cut, N), in_=runs(dy_raw, cut, N), func=ACT.Copy)
+        quantise(nc, dy_codes, dy_scales, dy_bf, E5M2, 0, N)
+
+        wo_dst = wo_bf[:].rearrange("p (t m j) -> p m j t", t=PACK, j=PACK)
+        wo_hi_dst = wo_hi[:].rearrange("p (t m j) -> p m j t", t=PACK, j=PACK)
+        for a in range(2):
+            wo_src = wo_raw[a][:].rearrange("p j (m t) -> p m j t", t=PACK)
+            ms = slice(a * P // 2, (a + 1) * P // 2)
+            nc.vector.tensor_copy(out=wo_dst[:, ms, :, 0:2], in_=wo_src[:, :, :, 0:2])
+            nc.scalar.activation(out=wo_hi_dst[:, ms, :, 2:4], in_=wo_src[:, :, :, 2:4], func=ACT.Copy)
+        quantise(nc, wo_codes, wo_scales, wo_bf, E4M3, 0, P)
+        quantise(nc, wo_codes, wo_scales, wo_bf, E4M3, P, 2 * P)
+        quantise(nc, wo_codes, wo_scales, wo_hi, E4M3, 2 * P, N)
+
+        u = []
+        for t in range(PACK):
+            bank = ps.tile([P, N], F32, name="u_bank%d" % t)
+            cols = slice(t * P, (t + 1) * P)
+            nc.tensor.matmul_mx(
+                out=bank[:],
+                lhsT=wo_codes[:, cols].bitcast(E4M3),
+                lhsT_scale=wo_scales[:, cols],
+                rhs=dy_codes[:].bitcast(E5M2),
+                rhs_scale=dy_scales[:],
+                start=True,
+                stop=True,
+            )
+            u_t = sb.tile([P, N], F32, name="u%d" % t)
+            nc.scalar.copy(out=u_t[:], in_=bank[:])
+            u.append(u_t)
+
+        neg_u = [sb.tile([P, PACK, HALF], F32, name="neg_u%d" % a) for a in range(2)]
+        for a in range(2):
+            lists = offsets[:, a * HALF // 16 : (a + 1) * HALF // 16]
+            for t in range(PACK):
+                nc.vector.tensor_scalar(
+                    out=neg_u[a][:, t, :],
+                    in0=u[t][:].indirect(lists),
+                    scalar1=-1.0,
+                    scalar2=0.0,
+                    op0=ALU.mult,
+                    op1=ALU.add,
+                )
+
+        h_sq = sb.tile([P, N * PACK], F32, name="h_sq")
+        for a in range(2):
+            nc.scalar.activation(
+                out=weave(h_sq, a * HALF, (a + 1) * HALF), in_=runs(h_raw, a * HALF, (a + 1) * HALF), func=ACT.Square
+            )
+
+        w_dst = w_bf[:].rearrange("p (t m j) -> p m j t", t=PACK, j=PACK)
+        w_src = w_raw[:].rearrange("p j (m t) -> p m j t", t=PACK)
+        nc.scalar.activation(out=w_dst, in_=w_src, func=ACT.Copy)
+
+        def through_tanh(c0, c1):
+            a = c0 // HALF
+            nc.vector.scalar_tensor_tensor(
+                out=dz_bf[:, c0 * PACK : c1 * PACK].rearrange("p (c j) -> p c j", j=PACK),
+                in0=h_sq[:, c0 * PACK : c1 * PACK].rearrange("p (c j) -> p c j", j=PACK),
+                scalar=1.0,
+                in1=neg_u[a][:, :, c0 - a * HALF : c1 - a * HALF].rearrange("p j c -> p c j"),
+                op0=ALU.subtract,
+                op1=ALU.mult,
+            )
+
+        through_tanh(0, 256)
+        through_tanh(256, 384)
+        quantise(nc, dz_codes, dz_scales, dz_bf, E5M2, 0, 256)
+        through_tanh(384, 512)
+        quantise(nc, w_codes, w_scales, w_bf, E4M3, 0, N)
+        quantise(nc, dz_codes, dz_scales, dz_bf, E5M2, 256, 512)
+
+        y_lo = sb.tile([P, 2, N], F32, name="y_lo")
+        y_hi = [sb.tile([P, 2, HALF], F32, name="y_hi%d" % a) for a in range(2)]
+        y_rows = out_0.rearrange("(p t) c -> p t c", t=PACK)
+        y_words = y_bf[:].rearrange("p (c t) -> p c t", t=PACK)
+        banks = []
+        for t in range(PACK):
+            bank = ps.tile([P, N], F32, name="y_bank%d" % t)
+            cols = slice(t * P, (t + 1) * P)
+            nc.tensor.matmul_mx(
+                out=bank[:],
+                lhsT=w_codes[:, cols].bitcast(E4M3),
+                lhsT_scale=w_scales[:, cols],
+                rhs=dz_codes[:].bitcast(E5M2),
+                rhs_scale=dz_scales[:],
+                start=True,
+                stop=True,
+            )
+            banks.append(bank)
+        nc.scalar.copy(out=y_lo[:, 0, :], in_=banks[0][:])
+        nc.vector.tensor_copy(out=y_lo[:, 1, :], in_=banks[1][:])
+        nc.sync.dma_start(out=y_rows[:, 0:2, :], in_=y_lo[:])
+        nc.vector.tensor_copy(out=y_words[:, :, 0:2], in_=y_lo[:].rearrange("p t c -> p c t"))
+        for t in range(2, PACK):
+            for a in range(2):
+                nc.scalar.copy(out=y_hi[a][:, t - 2, :], in_=banks[t][:, a * HALF : (a + 1) * HALF])
+        for a in range(2):
+            nc.sync.dma_start(out=y_rows[:, 2:4, a * HALF : (a + 1) * HALF], in_=y_hi[a][:])
+            nc.vector.tensor_copy(
+                out=y_words[:, a * HALF : (a + 1) * HALF, 2:4], in_=y_hi[a][:].rearrange("p t c -> p c t")
+            )
+        words = out_1.rearrange("g p c l -> (g p) (c l)").bitcast(I32)
+        for a in range(2):
+            quantise(nc, y_codes, y_scales, y_bf, E4M3, a * HALF, (a + 1) * HALF)
+            nc.sync.dma_start(
+                out=words[:, a * HALF : (a + 1) * HALF], in_=y_codes[:, a * HALF : (a + 1) * HALF].bitcast(I32)
+            )
+        rows = out_2.rearrange("g q c -> (g q) c").bitcast(I32)
+        for q in range(4):
+            engine = nc.scalar if q % 2 == 0 else nc.sync
+            engine.dma_start(out=rows[4 * q : 4 * q + 4, :], in_=y_scales[32 * q : 32 * q + 4, :].bitcast(I32))

@@ -37,20 +37,24 @@ def tile_attend_ghsort_tnh_pl_kernel(tc, wo, dyT, W, h, offs, out_0, out_1, out_
         offsets = sb.tile([P, N // 16], U16, name="offsets")
         wo_raw = [sb.tile([P, PACK, HALF], F32, name="wo_raw%d" % a) for a in range(2)]
         dy_raw = sb.tile([P, PACK, N], F32, name="dy_raw")
-        h_raw = sb.tile([P, PACK, N], F32, name="h_raw")
-        w_raw = sb.tile([P, PACK, N], F32, name="w_raw")
+        h_raw = [sb.tile([P, PACK, HALF], F32, name="h_raw%d" % a) for a in range(2)]
+        w_raw = [sb.tile([P, PACK, HALF], F32, name="w_raw%d" % a) for a in range(2)]
 
         nc.sync.dma_start(out=dy_raw[:], in_=dyT.rearrange("(p j) c -> p j c", j=PACK))
         wo_rows = wo.rearrange("(p j) c -> p j c", j=PACK)
         for a in range(2):
             nc.sync.dma_start(out=wo_raw[a][:], in_=wo_rows[:, :, a * HALF : (a + 1) * HALF])
         nc.sync.dma_start(offsets[:], offs)
-        nc.sync.dma_start(out=h_raw[:], in_=h.rearrange("(p j) c -> p j c", j=PACK))
-        nc.sync.dma_start(out=w_raw[:], in_=W.rearrange("(p j) c -> p j c", j=PACK))
+        w_rows = W.rearrange("(p j) c -> p j c", j=PACK)
+        h_rows = h.rearrange("(p j) c -> p j c", j=PACK)
+        nc.sync.dma_start(out=w_raw[0][:], in_=w_rows[:, :, 0:HALF])
+        nc.sync.dma_start(out=h_raw[0][:], in_=h_rows[:, :, 0:HALF])
+        nc.sync.dma_start(out=h_raw[1][:], in_=h_rows[:, :, HALF:N])
+        nc.sync.dma_start(out=w_raw[1][:], in_=w_rows[:, :, HALF:N])
 
         def operand(name):
             grouped = sb.tile([P, N * PACK], BF16, name=name + "_bf", align_bytes=64)
-            codes = sb.tile([P, N], U32, name=name + "_codes", align_bytes=64)
+            codes = sb.tile([P, N], U32, name=name + "_codes", tag=name + "_codes", align_bytes=64)
             scales = sb.tile([P, N], U8, name=name + "_scales", align_bytes=64)
             return grouped, codes, scales
 
@@ -100,38 +104,41 @@ def tile_attend_ghsort_tnh_pl_kernel(tc, wo, dyT, W, h, offs, out_0, out_1, out_
             nc.scalar.copy(out=u_t[:], in_=bank[:])
             u.append(u_t)
 
-        neg_u = [sb.tile([P, PACK, HALF], F32, name="neg_u%d" % a) for a in range(2)]
+        w_lo_dst = w_bf[:].rearrange("p (t m j) -> p m j t", t=PACK, j=PACK)
+        nc.vector.tensor_copy(
+            out=w_lo_dst[:, 0 : P // 2], in_=w_raw[0][:].rearrange("p j (m t) -> p m j t", t=PACK)
+        )
+
+        picked = [sb.tile([P, PACK, HALF], F32, name="picked%d" % a) for a in range(2)]
         for a in range(2):
             lists = offsets[:, a * HALF // 16 : (a + 1) * HALF // 16]
             for t in range(PACK):
-                nc.vector.tensor_scalar(
-                    out=neg_u[a][:, t, :],
-                    in0=u[t][:].indirect(lists),
-                    scalar1=-1.0,
-                    scalar2=0.0,
-                    op0=ALU.mult,
-                    op1=ALU.add,
-                )
+                nc.vector.tensor_copy(out=picked[a][:, t, :], in_=u[t][:].indirect(lists))
 
-        h_sq = sb.tile([P, N * PACK], F32, name="h_sq")
-        for a in range(2):
+        h_sq = []
+        for a, spent in enumerate(("dy_codes", "wo_codes")):
+            square = sb.tile([P, HALF * PACK], F32, name="h_sq%d" % a, tag=spent, align_bytes=64)
             nc.scalar.activation(
-                out=weave(h_sq, a * HALF, (a + 1) * HALF), in_=runs(h_raw, a * HALF, (a + 1) * HALF), func=ACT.Square
+                out=square[:].rearrange("p (c j i) -> p c j i", j=PACK, i=4), in_=runs(h_raw[a], 0, HALF), func=ACT.Square
             )
-
-        w_dst = w_bf[:].rearrange("p (t m j) -> p m j t", t=PACK, j=PACK)
-        w_src = w_raw[:].rearrange("p j (m t) -> p m j t", t=PACK)
-        nc.scalar.activation(out=w_dst, in_=w_src, func=ACT.Copy)
+            h_sq.append(square)
+        slope = [sb.tile([P, HALF * PACK], F32, name="slope%d" % a) for a in range(2)]
+        for a in range(2):
+            nc.scalar.activation(out=slope[a][:], in_=h_sq[a][:], func=ACT.Identity, scale=-1.0, bias=1.0)
+        nc.scalar.activation(
+            out=w_lo_dst[:, P // 2 : P],
+            in_=w_raw[1][:].rearrange("p j (m t) -> p m j t", t=PACK),
+            func=ACT.Copy,
+        )
 
         def through_tanh(c0, c1):
             a = c0 // HALF
-            nc.vector.scalar_tensor_tensor(
-                out=dz_bf[:, c0 * PACK : c1 * PACK].rearrange("p (c j) -> p c j", j=PACK),
-                in0=h_sq[:, c0 * PACK : c1 * PACK].rearrange("p (c j) -> p c j", j=PACK),
-                scalar=1.0,
-                in1=neg_u[a][:, :, c0 - a * HALF : c1 - a * HALF].rearrange("p j c -> p c j"),
-                op0=ALU.subtract,
-                op1=ALU.mult,
+            lo, hi = c0 - a * HALF, c1 - a * HALF
+            nc.vector.tensor_tensor(
+                out=weave(dz_bf, c0, c1),
+                in0=runs(picked[a], lo, hi),
+                in1=slope[a][:, lo * PACK : hi * PACK].rearrange("p (c j i) -> p c j i", j=PACK, i=4),
+                op=ALU.mult,
             )
 
         through_tanh(0, 256)
@@ -142,7 +149,7 @@ def tile_attend_ghsort_tnh_pl_kernel(tc, wo, dyT, W, h, offs, out_0, out_1, out_
         quantise(nc, dz_codes, dz_scales, dz_bf, E5M2, 256, 512)
 
         y_lo = sb.tile([P, 2, N], F32, name="y_lo")
-        y_hi = [sb.tile([P, 2, HALF], F32, name="y_hi%d" % a) for a in range(2)]
+        y_hi = sb.tile([P, 2, N], F32, name="y_hi")
         y_rows = out_0.rearrange("(p t) c -> p t c", t=PACK)
         y_words = y_bf[:].rearrange("p (c t) -> p c t", t=PACK)
         banks = []
@@ -163,14 +170,12 @@ def tile_attend_ghsort_tnh_pl_kernel(tc, wo, dyT, W, h, offs, out_0, out_1, out_
         nc.vector.tensor_copy(out=y_lo[:, 1, :], in_=banks[1][:])
         nc.sync.dma_start(out=y_rows[:, 0:2, :], in_=y_lo[:])
         nc.vector.tensor_copy(out=y_words[:, :, 0:2], in_=y_lo[:].rearrange("p t c -> p c t"))
-        for t in range(2, PACK):
-            for a in range(2):
-                nc.scalar.copy(out=y_hi[a][:, t - 2, :], in_=banks[t][:, a * HALF : (a + 1) * HALF])
+        nc.scalar.copy(out=y_hi[:, 0, :], in_=banks[2][:])
         for a in range(2):
-            nc.sync.dma_start(out=y_rows[:, 2:4, a * HALF : (a + 1) * HALF], in_=y_hi[a][:])
-            nc.vector.tensor_copy(
-                out=y_words[:, a * HALF : (a + 1) * HALF, 2:4], in_=y_hi[a][:].rearrange("p t c -> p c t")
-            )
+            tokens = slice(a * HALF, (a + 1) * HALF)
+            nc.scalar.copy(out=y_hi[:, 1, tokens], in_=banks[3][:, tokens])
+            nc.vector.tensor_copy(out=y_words[:, tokens, 2:4], in_=y_hi[:, :, tokens].rearrange("p t c -> p c t"))
+        nc.sync.dma_start(out=y_rows[:, 2:4, :], in_=y_hi[:])
         words = out_1.rearrange("g p c l -> (g p) (c l)").bitcast(I32)
         for a in range(2):
             quantise(nc, y_codes, y_scales, y_bf, E4M3, a * HALF, (a + 1) * HALF)

@@ -37,20 +37,20 @@ def tile_attend_ghsort_tnh_pl_kernel(tc, wo, dyT, W, h, offs, out_0, out_1, out_
         offsets = sb.tile([P, N // 16], U16, name="offsets")
         wo_raw = [sb.tile([P, PACK, HALF], F32, name="wo_raw%d" % a) for a in range(2)]
         dy_raw = sb.tile([P, PACK, N], F32, name="dy_raw")
-        h_raw = [sb.tile([P, PACK, HALF], F32, name="h_raw%d" % a) for a in range(2)]
-        w_raw = [sb.tile([P, PACK, HALF], F32, name="w_raw%d" % a) for a in range(2)]
+        h_head = sb.tile([P, PACK, P], F32, name="h_head")
+        h_rest = sb.tile([P, PACK, N - P], F32, name="h_rest")
+        w_raw = sb.tile([P, PACK, N], F32, name="w_raw")
 
         nc.sync.dma_start(out=dy_raw[:], in_=dyT.rearrange("(p j) c -> p j c", j=PACK))
         wo_rows = wo.rearrange("(p j) c -> p j c", j=PACK)
         for a in range(2):
             nc.sync.dma_start(out=wo_raw[a][:], in_=wo_rows[:, :, a * HALF : (a + 1) * HALF])
-        nc.sync.dma_start(offsets[:], offs)
         w_rows = W.rearrange("(p j) c -> p j c", j=PACK)
         h_rows = h.rearrange("(p j) c -> p j c", j=PACK)
-        nc.sync.dma_start(out=w_raw[0][:], in_=w_rows[:, :, 0:HALF])
-        nc.sync.dma_start(out=h_raw[0][:], in_=h_rows[:, :, 0:HALF])
-        nc.sync.dma_start(out=h_raw[1][:], in_=h_rows[:, :, HALF:N])
-        nc.sync.dma_start(out=w_raw[1][:], in_=w_rows[:, :, HALF:N])
+        nc.sync.dma_start(out=h_head[:], in_=h_rows[:, :, 0:P])
+        nc.sync.dma_start(offsets[:], offs)
+        nc.sync.dma_start(out=h_rest[:], in_=h_rows[:, :, P:N])
+        nc.sync.dma_start(out=w_raw[:], in_=w_rows)
 
         def operand(name):
             grouped = sb.tile([P, N * PACK], BF16, name=name + "_bf", align_bytes=64)
@@ -81,11 +81,33 @@ def tile_attend_ghsort_tnh_pl_kernel(tc, wo, dyT, W, h, offs, out_0, out_1, out_
         for a in range(2):
             wo_src = wo_raw[a][:].rearrange("p j (m t) -> p m j t", t=PACK)
             ms = slice(a * P // 2, (a + 1) * P // 2)
-            nc.vector.tensor_copy(out=wo_dst[:, ms, :, 0:2], in_=wo_src[:, :, :, 0:2])
+            if a == 0:
+                nc.vector.tensor_copy(out=wo_dst[:, ms, :, 0:2], in_=wo_src[:, :, :, 0:2])
+            else:
+                nc.vector.tensor_copy(out=wo_dst[:, 64:96, :, 0:2], in_=wo_src[:, 0:32, :, 0:2])
+                nc.scalar.activation(out=wo_dst[:, 96:128, :, 0:2], in_=wo_src[:, 32:64, :, 0:2], func=ACT.Copy)
             nc.scalar.activation(out=wo_hi_dst[:, ms, :, 2:4], in_=wo_src[:, :, :, 2:4], func=ACT.Copy)
         quantise(nc, wo_codes, wo_scales, wo_bf, E4M3, 0, P)
         quantise(nc, wo_codes, wo_scales, wo_bf, E4M3, P, 2 * P)
         quantise(nc, wo_codes, wo_scales, wo_hi, E4M3, 2 * P, N)
+
+        slope = sb.tile([P, N * PACK], F32, name="slope")
+
+        def square(raw, c0, c1, tag):
+            tile = sb.tile([P, (c1 - c0) * PACK], F32, name="h_sq_" + tag, tag=tag, align_bytes=64)
+            nc.scalar.activation(
+                out=tile[:].rearrange("p (c j i) -> p c j i", j=PACK, i=4), in_=runs(raw, c0, c1), func=ACT.Square
+            )
+            return tile
+
+        nc.vector.tensor_scalar(
+            out=slope[:, 0 : P * PACK],
+            in0=square(h_head, 0, P, "head")[:],
+            scalar1=-1.0,
+            scalar2=1.0,
+            op0=ALU.mult,
+            op1=ALU.add,
+        )
 
         u = []
         for t in range(PACK):
@@ -100,53 +122,36 @@ def tile_attend_ghsort_tnh_pl_kernel(tc, wo, dyT, W, h, offs, out_0, out_1, out_
                 start=True,
                 stop=True,
             )
-            u_t = sb.tile([P, N], F32, name="u%d" % t)
-            nc.scalar.copy(out=u_t[:], in_=bank[:])
+            u_t = sb.tile([P, 2 * N], F32, name="u%d" % t)
+            nc.vector.memset(u_t[:, N : 2 * N], 0.0)
+            nc.scalar.copy(out=u_t[:, 0:N], in_=bank[:])
             u.append(u_t)
 
-        w_lo_dst = w_bf[:].rearrange("p (t m j) -> p m j t", t=PACK, j=PACK)
-        nc.vector.tensor_copy(
-            out=w_lo_dst[:, 0 : P // 2], in_=w_raw[0][:].rearrange("p j (m t) -> p m j t", t=PACK)
-        )
+        picked = sb.tile([P, PACK, N], F32, name="picked")
+        for t in range(PACK):
+            nc.vector.tensor_copy(out=picked[:, t, :], in_=u[t][:].indirect(offsets[:]))
 
-        picked = [sb.tile([P, PACK, HALF], F32, name="picked%d" % a) for a in range(2)]
-        for a in range(2):
-            lists = offsets[:, a * HALF // 16 : (a + 1) * HALF // 16]
-            for t in range(PACK):
-                nc.vector.tensor_copy(out=picked[a][:, t, :], in_=u[t][:].indirect(lists))
+        h_sq = [square(h_rest, 0, P, "dy_codes"), square(h_rest, P, N - P, "wo_codes")]
+        nc.scalar.activation(out=slope[:, P * PACK : HALF * PACK], in_=h_sq[0][:], func=ACT.Identity, scale=-1.0, bias=1.0)
+        nc.scalar.activation(out=slope[:, HALF * PACK : N * PACK], in_=h_sq[1][:], func=ACT.Identity, scale=-1.0, bias=1.0)
 
-        h_sq = []
-        for a, spent in enumerate(("dy_codes", "wo_codes")):
-            square = sb.tile([P, HALF * PACK], F32, name="h_sq%d" % a, tag=spent, align_bytes=64)
-            nc.scalar.activation(
-                out=square[:].rearrange("p (c j i) -> p c j i", j=PACK, i=4), in_=runs(h_raw[a], 0, HALF), func=ACT.Square
-            )
-            h_sq.append(square)
-        slope = [sb.tile([P, HALF * PACK], F32, name="slope%d" % a) for a in range(2)]
-        for a in range(2):
-            nc.scalar.activation(out=slope[a][:], in_=h_sq[a][:], func=ACT.Identity, scale=-1.0, bias=1.0)
-        nc.scalar.activation(
-            out=w_lo_dst[:, P // 2 : P],
-            in_=w_raw[1][:].rearrange("p j (m t) -> p m j t", t=PACK),
-            func=ACT.Copy,
-        )
+        w_dst = w_bf[:].rearrange("p (t m j) -> p m j t", t=PACK, j=PACK)
+        w_src = w_raw[:].rearrange("p j (m t) -> p m j t", t=PACK)
+        for t in (0, 2):
+            nc.scalar.activation(out=w_dst[:, :, :, t : t + 2], in_=w_src[:, :, :, t : t + 2], func=ACT.Copy)
 
-        def through_tanh(c0, c1):
-            a = c0 // HALF
-            lo, hi = c0 - a * HALF, c1 - a * HALF
+        for c0 in (0, HALF):
             nc.vector.tensor_tensor(
-                out=weave(dz_bf, c0, c1),
-                in0=runs(picked[a], lo, hi),
-                in1=slope[a][:, lo * PACK : hi * PACK].rearrange("p (c j i) -> p c j i", j=PACK, i=4),
+                out=weave(dz_bf, c0, c0 + HALF),
+                in0=runs(picked, c0, c0 + HALF),
+                in1=slope[:, c0 * PACK : (c0 + HALF) * PACK].rearrange("p (c j i) -> p c j i", j=PACK, i=4),
                 op=ALU.mult,
             )
-
-        through_tanh(0, 256)
-        through_tanh(256, 384)
-        quantise(nc, dz_codes, dz_scales, dz_bf, E5M2, 0, 256)
-        through_tanh(384, 512)
-        quantise(nc, w_codes, w_scales, w_bf, E4M3, 0, N)
-        quantise(nc, dz_codes, dz_scales, dz_bf, E5M2, 256, 512)
+        quantise(nc, dz_codes, dz_scales, dz_bf, E5M2, 0, HALF)
+        quantise(nc, w_codes, w_scales, w_bf, E4M3, 0, P)
+        quantise(nc, dz_codes, dz_scales, dz_bf, E5M2, HALF, N)
+        quantise(nc, w_codes, w_scales, w_bf, E4M3, P, 2 * P)
+        quantise(nc, w_codes, w_scales, w_bf, E4M3, 2 * P, N)
 
         y_lo = sb.tile([P, 2, N], F32, name="y_lo")
         y_hi = sb.tile([P, 2, N], F32, name="y_hi")
@@ -166,16 +171,20 @@ def tile_attend_ghsort_tnh_pl_kernel(tc, wo, dyT, W, h, offs, out_0, out_1, out_
                 stop=True,
             )
             banks.append(bank)
-        nc.scalar.copy(out=y_lo[:, 0, :], in_=banks[0][:])
-        nc.vector.tensor_copy(out=y_lo[:, 1, :], in_=banks[1][:])
-        nc.sync.dma_start(out=y_rows[:, 0:2, :], in_=y_lo[:])
+        nc.vector.tensor_copy(out=y_lo[:, 0, :], in_=banks[0][:])
+        nc.sync.dma_start(out=y_rows[:, 0, :], in_=y_lo[:, 0, :])
+        nc.scalar.copy(out=y_lo[:, 1, :], in_=banks[1][:])
+        nc.sync.dma_start(out=y_rows[:, 1, :], in_=y_lo[:, 1, :])
         nc.vector.tensor_copy(out=y_words[:, :, 0:2], in_=y_lo[:].rearrange("p t c -> p c t"))
         nc.scalar.copy(out=y_hi[:, 0, :], in_=banks[2][:])
-        for a in range(2):
-            tokens = slice(a * HALF, (a + 1) * HALF)
+        nc.sync.dma_start(out=y_rows[:, 2, :], in_=y_hi[:, 0, :])
+        first, second, third = slice(0, 256), slice(256, 384), slice(384, 512)
+        for tokens in (first, third, second):
             nc.scalar.copy(out=y_hi[:, 1, tokens], in_=banks[3][:, tokens])
+        for tokens in (first, second):
             nc.vector.tensor_copy(out=y_words[:, tokens, 2:4], in_=y_hi[:, :, tokens].rearrange("p t c -> p c t"))
-        nc.sync.dma_start(out=y_rows[:, 2:4, :], in_=y_hi[:])
+        nc.scalar.copy(out=y_words[:, third, 2:4], in_=y_hi[:, :, third].rearrange("p t c -> p c t"))
+        nc.sync.dma_start(out=y_rows[:, 3, :], in_=y_hi[:, 1, :])
         words = out_1.rearrange("g p c l -> (g p) (c l)").bitcast(I32)
         for a in range(2):
             quantise(nc, y_codes, y_scales, y_bf, E4M3, a * HALF, (a + 1) * HALF)

@@ -55,7 +55,7 @@ def tile_attend_ghsort_tnh_pl_kernel(tc, wo, dyT, W, h, offs, out_0, out_1, out_
         def operand(name):
             grouped = sb.tile([P, N * PACK], BF16, name=name + "_bf", align_bytes=64)
             codes = sb.tile([P, N], U32, name=name + "_codes", tag=name + "_codes", align_bytes=64)
-            scales = sb.tile([P, N], U8, name=name + "_scales", align_bytes=64)
+            scales = sb.tile([P, N], U8, name=name + "_scales", tag=name + "_scales", align_bytes=64)
             return grouped, codes, scales
 
         wo_bf, wo_codes, wo_scales = operand("wo")
@@ -110,6 +110,7 @@ def tile_attend_ghsort_tnh_pl_kernel(tc, wo, dyT, W, h, offs, out_0, out_1, out_
         )
 
         u = []
+        u_banks = []
         for t in range(PACK):
             bank = ps.tile([P, N], F32, name="u_bank%d" % t)
             cols = slice(t * P, (t + 1) * P)
@@ -126,12 +127,13 @@ def tile_attend_ghsort_tnh_pl_kernel(tc, wo, dyT, W, h, offs, out_0, out_1, out_
             nc.vector.memset(u_t[:, N : 2 * N], 0.0)
             nc.scalar.copy(out=u_t[:, 0:N], in_=bank[:])
             u.append(u_t)
+            u_banks.append(bank)
 
         picked = sb.tile([P, PACK, N], F32, name="picked")
         for t in range(PACK):
             nc.vector.tensor_copy(out=picked[:, t, :], in_=u[t][:].indirect(offsets[:]))
 
-        h_sq = [square(h_rest, 0, P, "dy_codes"), square(h_rest, P, N - P, "wo_codes")]
+        h_sq = [square(h_rest, 0, P, "dy_codes"), square(h_rest, P, N - P, "dy_scales")]
         nc.scalar.activation(out=slope[:, P * PACK : HALF * PACK], in_=h_sq[0][:], func=ACT.Identity, scale=-1.0, bias=1.0)
         nc.scalar.activation(out=slope[:, HALF * PACK : N * PACK], in_=h_sq[1][:], func=ACT.Identity, scale=-1.0, bias=1.0)
 
@@ -140,14 +142,29 @@ def tile_attend_ghsort_tnh_pl_kernel(tc, wo, dyT, W, h, offs, out_0, out_1, out_
         for t in (0, 2):
             nc.scalar.activation(out=w_dst[:, :, :, t : t + 2], in_=w_src[:, :, :, t : t + 2], func=ACT.Copy)
 
-        for c0 in (0, HALF):
+        def through_tanh(c0, c1):
             nc.vector.tensor_tensor(
-                out=weave(dz_bf, c0, c0 + HALF),
-                in0=runs(picked, c0, c0 + HALF),
-                in1=slope[:, c0 * PACK : (c0 + HALF) * PACK].rearrange("p (c j i) -> p c j i", j=PACK, i=4),
+                out=weave(dz_bf, c0, c1),
+                in0=runs(picked, c0, c1),
+                in1=slope[:, c0 * PACK : c1 * PACK].rearrange("p (c j i) -> p c j i", j=PACK, i=4),
                 op=ALU.mult,
             )
-        quantise(nc, dz_codes, dz_scales, dz_bf, E5M2, 0, HALF)
+
+        through_tanh(0, 192)
+        through_tanh(192, HALF)
+        quantise(nc, dz_codes, dz_scales, dz_bf, E5M2, 0, P)
+        for bank in u_banks[0:2]:
+            nc.tensor.matmul_mx(
+                out=bank[:],
+                lhsT=dz_codes[:, 0:P].bitcast(E5M2),
+                lhsT_scale=dz_scales[:, 0:P],
+                rhs=wo_codes[:].bitcast(E4M3),
+                rhs_scale=wo_scales[:],
+                start=True,
+                stop=True,
+            )
+        through_tanh(HALF, N)
+        quantise(nc, dz_codes, dz_scales, dz_bf, E5M2, P, HALF)
         quantise(nc, w_codes, w_scales, w_bf, E4M3, 0, P)
         quantise(nc, dz_codes, dz_scales, dz_bf, E5M2, HALF, N)
         quantise(nc, w_codes, w_scales, w_bf, E4M3, P, 2 * P)

@@ -5,8 +5,8 @@ import concourse.mybir as mybir
 F32 = mybir.dt.float32
 BF16 = mybir.dt.bfloat16
 I32 = mybir.dt.int32
-U32 = mybir.dt.uint32
 U16 = mybir.dt.uint16
+U32 = mybir.dt.uint32
 U8 = mybir.dt.uint8
 E4M3 = mybir.dt.float8_e4m3fn_x4
 E5M2 = mybir.dt.float8_e5m2_x4
@@ -20,12 +20,20 @@ HALF = N // 2
 FLOPS = 2 * 2 * N * N * N
 
 
-def quantise(nc, codes, scales, grouped, fmt, c0, c1):
+def quantise(nc, codes, scales, grouped, fmt, c0, c1, shift=0):
     nc.vector.quantize_mx(
-        out=codes[:, c0:c1].bitcast(fmt),
-        scales=scales[:, c0:c1],
+        out=codes[:, shift + c0 : shift + c1].bitcast(fmt),
+        scales=scales[:, shift + c0 : shift + c1],
         in_=grouped[:, c0 * PACK : c1 * PACK],
     )
+
+
+def weave(tile, c0, c1):
+    return tile[:, c0 * PACK : c1 * PACK].rearrange("p (c i j) -> p c j i", i=4, j=PACK)
+
+
+def runs(planes, c0, c1):
+    return planes[:, :, c0:c1].rearrange("p j (c i) -> p c j i", i=4)
 
 
 def tile_attend_ghsort_tnh_pl_kernel(tc, wo, dyT, W, h, offs, out_0, out_1, out_2):
@@ -35,22 +43,20 @@ def tile_attend_ghsort_tnh_pl_kernel(tc, wo, dyT, W, h, offs, out_0, out_1, out_
         ps = ctx.enter_context(tc.psum_pool(name="ps", bufs=1))
 
         offsets = sb.tile([P, N // 16], U16, name="offsets")
-        wo_raw = [sb.tile([P, PACK, HALF], F32, name="wo_raw%d" % a) for a in range(2)]
+        wo_raw = sb.tile([P, PACK, N], F32, name="wo_raw")
         dy_raw = sb.tile([P, PACK, N], F32, name="dy_raw")
-        h_head = sb.tile([P, PACK, P], F32, name="h_head")
-        h_rest = sb.tile([P, PACK, N - P], F32, name="h_rest")
+        h_head = sb.tile([P, N], F32, name="h_head")
+        h_rest = sb.tile([P, PACK - 1, N], F32, name="h_rest")
         w_raw = sb.tile([P, PACK, N], F32, name="w_raw")
 
-        nc.sync.dma_start(out=dy_raw[:], in_=dyT.rearrange("(p j) c -> p j c", j=PACK))
-        wo_rows = wo.rearrange("(p j) c -> p j c", j=PACK)
-        for a in range(2):
-            nc.sync.dma_start(out=wo_raw[a][:], in_=wo_rows[:, :, a * HALF : (a + 1) * HALF])
-        w_rows = W.rearrange("(p j) c -> p j c", j=PACK)
         h_rows = h.rearrange("(p j) c -> p j c", j=PACK)
-        nc.sync.dma_start(out=h_head[:], in_=h_rows[:, :, 0:P])
+        wo_rows = wo.rearrange("(p j) c -> p j c", j=PACK)
+        nc.sync.dma_start(out=dy_raw[:], in_=dyT.rearrange("(p j) c -> p j c", j=PACK))
+        nc.sync.dma_start(out=wo_raw[:], in_=wo_rows)
+        nc.sync.dma_start(out=h_head[:], in_=h_rows[:, 0, :])
         nc.sync.dma_start(offsets[:], offs)
-        nc.sync.dma_start(out=h_rest[:], in_=h_rows[:, :, P:N])
-        nc.sync.dma_start(out=w_raw[:], in_=w_rows)
+        nc.sync.dma_start(out=h_rest[:], in_=h_rows[:, 1:PACK, :])
+        nc.sync.dma_start(out=w_raw[:], in_=W.rearrange("(p j) c -> p j c", j=PACK))
 
         def operand(name):
             grouped = sb.tile([P, N * PACK], BF16, name=name + "_bf", align_bytes=64)
@@ -59,17 +65,10 @@ def tile_attend_ghsort_tnh_pl_kernel(tc, wo, dyT, W, h, offs, out_0, out_1, out_
             return grouped, codes, scales
 
         wo_bf, wo_codes, wo_scales = operand("wo")
-        wo_hi = sb.tile([P, N * PACK], BF16, name="wo_hi", align_bytes=64)
         dy_bf, dy_codes, dy_scales = operand("dy")
         w_bf, w_codes, w_scales = operand("w")
         dz_bf, dz_codes, dz_scales = operand("dz")
         y_bf, y_codes, y_scales = operand("y")
-
-        def weave(tile, c0, c1):
-            return tile[:, c0 * PACK : c1 * PACK].rearrange("p (c i j) -> p c j i", i=4, j=PACK)
-
-        def runs(raw, c0, c1):
-            return raw[:, :, c0:c1].rearrange("p j (c i) -> p c j i", i=4)
 
         cut = 320
         nc.vector.tensor_copy(out=weave(dy_bf, 0, cut), in_=runs(dy_raw, 0, cut))
@@ -77,36 +76,20 @@ def tile_attend_ghsort_tnh_pl_kernel(tc, wo, dyT, W, h, offs, out_0, out_1, out_
         quantise(nc, dy_codes, dy_scales, dy_bf, E5M2, 0, N)
 
         wo_dst = wo_bf[:].rearrange("p (t m j) -> p m j t", t=PACK, j=PACK)
-        wo_hi_dst = wo_hi[:].rearrange("p (t m j) -> p m j t", t=PACK, j=PACK)
-        for a in range(2):
-            wo_src = wo_raw[a][:].rearrange("p j (m t) -> p m j t", t=PACK)
-            ms = slice(a * P // 2, (a + 1) * P // 2)
-            if a == 0:
-                nc.vector.tensor_copy(out=wo_dst[:, ms, :, 0:2], in_=wo_src[:, :, :, 0:2])
-            else:
-                nc.vector.tensor_copy(out=wo_dst[:, 64:96, :, 0:2], in_=wo_src[:, 0:32, :, 0:2])
-                nc.scalar.activation(out=wo_dst[:, 96:128, :, 0:2], in_=wo_src[:, 32:64, :, 0:2], func=ACT.Copy)
-            nc.scalar.activation(out=wo_hi_dst[:, ms, :, 2:4], in_=wo_src[:, :, :, 2:4], func=ACT.Copy)
+        wo_src = wo_raw[:].rearrange("p j (m t) -> p m j t", t=PACK)
+        mcut = 92
+        nc.vector.tensor_copy(out=wo_dst[:, 0:mcut, :, 0:2], in_=wo_src[:, 0:mcut, :, 0:2])
+        nc.scalar.activation(out=wo_dst[:, mcut:P, :, 0:2], in_=wo_src[:, mcut:P, :, 0:2], func=ACT.Copy)
         quantise(nc, wo_codes, wo_scales, wo_bf, E4M3, 0, P)
         quantise(nc, wo_codes, wo_scales, wo_bf, E4M3, P, 2 * P)
-        quantise(nc, wo_codes, wo_scales, wo_hi, E4M3, 2 * P, N)
+        nc.vector.tensor_copy(out=wo_dst[:, :, :, 2:4], in_=wo_src[:, :, :, 2:4])
+        quantise(nc, wo_codes, wo_scales, wo_bf, E4M3, 2 * P, N)
 
-        slope = sb.tile([P, N * PACK], F32, name="slope")
-
-        def square(raw, c0, c1, tag):
-            tile = sb.tile([P, (c1 - c0) * PACK], F32, name="h_sq_" + tag, tag=tag, align_bytes=64)
-            nc.scalar.activation(
-                out=tile[:].rearrange("p (c j i) -> p c j i", j=PACK, i=4), in_=runs(raw, c0, c1), func=ACT.Square
-            )
-            return tile
-
+        slope = sb.tile([P, PACK, N], F32, name="slope")
+        sq_head = sb.tile([P, N], F32, name="sq_head")
+        nc.scalar.activation(out=sq_head[:], in_=h_head[:], func=ACT.Square)
         nc.vector.tensor_scalar(
-            out=slope[:, 0 : P * PACK],
-            in0=square(h_head, 0, P, "head")[:],
-            scalar1=-1.0,
-            scalar2=1.0,
-            op0=ALU.mult,
-            op1=ALU.add,
+            out=slope[:, 0, :], in0=sq_head[:], scalar1=-1.0, scalar2=1.0, op0=ALU.mult, op1=ALU.add
         )
 
         u = []
@@ -133,9 +116,13 @@ def tile_attend_ghsort_tnh_pl_kernel(tc, wo, dyT, W, h, offs, out_0, out_1, out_
         for t in range(PACK):
             nc.vector.tensor_copy(out=picked[:, t, :], in_=u[t][:].indirect(offsets[:]))
 
-        h_sq = [square(h_rest, 0, P, "dy_codes"), square(h_rest, P, N - P, "dy_scales")]
-        nc.scalar.activation(out=slope[:, P * PACK : HALF * PACK], in_=h_sq[0][:], func=ACT.Identity, scale=-1.0, bias=1.0)
-        nc.scalar.activation(out=slope[:, HALF * PACK : N * PACK], in_=h_sq[1][:], func=ACT.Identity, scale=-1.0, bias=1.0)
+        sq_rest = sb.tile([P, PACK - 1, N], F32, name="sq_rest", tag="dy_codes", align_bytes=64)
+        nc.scalar.activation(out=sq_rest[:], in_=h_rest[:], func=ACT.Square)
+        for a in range(2):
+            tokens = slice(a * HALF, (a + 1) * HALF)
+            nc.scalar.activation(
+                out=slope[:, 1:PACK, tokens], in_=sq_rest[:, :, tokens], func=ACT.Identity, scale=-1.0, bias=1.0
+            )
 
         w_dst = w_bf[:].rearrange("p (t m j) -> p m j t", t=PACK, j=PACK)
         w_src = w_raw[:].rearrange("p j (m t) -> p m j t", t=PACK)
@@ -144,10 +131,7 @@ def tile_attend_ghsort_tnh_pl_kernel(tc, wo, dyT, W, h, offs, out_0, out_1, out_
 
         def through_tanh(c0, c1):
             nc.vector.tensor_tensor(
-                out=weave(dz_bf, c0, c1),
-                in0=runs(picked, c0, c1),
-                in1=slope[:, c0 * PACK : c1 * PACK].rearrange("p (c j i) -> p c j i", j=PACK, i=4),
-                op=ALU.mult,
+                out=weave(dz_bf, c0, c1), in0=runs(picked, c0, c1), in1=runs(slope, c0, c1), op=ALU.mult
             )
 
         through_tanh(0, 192)

@@ -45,114 +45,164 @@ def tile_attend_ghsort_tnh_pl_kernel(tc, wo, dyT, W, h, offs, out_0, out_1, out_
         offsets = sb.tile([P, N // 16], U16, name="offsets")
         wo_raw = sb.tile([P, PACK, N], F32, name="wo_raw")
         dy_raw = sb.tile([P, PACK, N], F32, name="dy_raw")
-        h_head = sb.tile([P, N], F32, name="h_head")
-        h_rest = sb.tile([P, PACK - 1, N], F32, name="h_rest")
+        h_head = [sb.tile([P, N], F32, name="h_head%d" % j) for j in range(2)]
+        h_rest = sb.tile([P, 2, N], F32, name="h_rest")
         w_raw = sb.tile([P, PACK, N], F32, name="w_raw")
 
         h_rows = h.rearrange("(p j) c -> p j c", j=PACK)
-        wo_rows = wo.rearrange("(p j) c -> p j c", j=PACK)
         nc.sync.dma_start(out=dy_raw[:], in_=dyT.rearrange("(p j) c -> p j c", j=PACK))
-        nc.sync.dma_start(out=wo_raw[:], in_=wo_rows)
-        nc.sync.dma_start(out=h_head[:], in_=h_rows[:, 0, :])
+        nc.sync.dma_start(out=wo_raw[:], in_=wo.rearrange("(p j) c -> p j c", j=PACK))
+        for j in range(2):
+            nc.sync.dma_start(out=h_head[j][:], in_=h_rows[:, j, :])
         nc.sync.dma_start(offsets[:], offs)
-        nc.sync.dma_start(out=h_rest[:], in_=h_rows[:, 1:PACK, :])
+        nc.sync.dma_start(out=h_rest[:], in_=h_rows[:, 2:PACK, :])
         nc.sync.dma_start(out=w_raw[:], in_=W.rearrange("(p j) c -> p j c", j=PACK))
 
         def operand(name):
-            grouped = sb.tile([P, N * PACK], BF16, name=name + "_bf", align_bytes=64)
+            grouped = sb.tile([P, N * PACK], BF16, name=name + "_bf", tag=name + "_bf", align_bytes=64)
             codes = sb.tile([P, N], U32, name=name + "_codes", tag=name + "_codes", align_bytes=64)
             scales = sb.tile([P, N], U8, name=name + "_scales", tag=name + "_scales", align_bytes=64)
             return grouped, codes, scales
 
-        wo_bf, wo_codes, wo_scales = operand("wo")
         dy_bf, dy_codes, dy_scales = operand("dy")
         w_bf, w_codes, w_scales = operand("w")
         dz_bf, dz_codes, dz_scales = operand("dz")
         y_bf, y_codes, y_scales = operand("y")
+        wo_bf = sb.tile([P, N * PACK], BF16, name="wo_bf", align_bytes=64)
+        wo_scales = sb.tile([P, N], U8, name="wo_scales", align_bytes=64)
+        wo_codes = [
+            sb.tile([P, width], U32, name="wo_codes", tag="wo_codes%d" % a, align_bytes=64)
+            for a, width in enumerate((P, P, HALF))
+        ]
+        wo_plane = [wo_codes[0][:], wo_codes[1][:], wo_codes[2][:, 0:P], wo_codes[2][:, P:HALF]]
 
         cut = 320
         nc.vector.tensor_copy(out=weave(dy_bf, 0, cut), in_=runs(dy_raw, 0, cut))
         nc.scalar.activation(out=weave(dy_bf, cut, N), in_=runs(dy_raw, cut, N), func=ACT.Copy)
         quantise(nc, dy_codes, dy_scales, dy_bf, E5M2, 0, N)
 
+        def quantise_wo(a, c0, c1):
+            nc.vector.quantize_mx(
+                out=wo_codes[a][:].bitcast(E4M3), scales=wo_scales[:, c0:c1], in_=wo_bf[:, c0 * PACK : c1 * PACK]
+            )
+
         wo_dst = wo_bf[:].rearrange("p (t m j) -> p m j t", t=PACK, j=PACK)
         wo_src = wo_raw[:].rearrange("p j (m t) -> p m j t", t=PACK)
         mcut = 92
         nc.vector.tensor_copy(out=wo_dst[:, 0:mcut, :, 0:2], in_=wo_src[:, 0:mcut, :, 0:2])
         nc.scalar.activation(out=wo_dst[:, mcut:P, :, 0:2], in_=wo_src[:, mcut:P, :, 0:2], func=ACT.Copy)
-        quantise(nc, wo_codes, wo_scales, wo_bf, E4M3, 0, P)
-        quantise(nc, wo_codes, wo_scales, wo_bf, E4M3, P, 2 * P)
+        quantise_wo(0, 0, P)
+        quantise_wo(1, P, HALF)
         nc.vector.tensor_copy(out=wo_dst[:, :, :, 2:4], in_=wo_src[:, :, :, 2:4])
-        quantise(nc, wo_codes, wo_scales, wo_bf, E4M3, 2 * P, N)
 
-        slope = sb.tile([P, PACK, N], F32, name="slope")
-        sq_head = sb.tile([P, N], F32, name="sq_head")
-        nc.scalar.activation(out=sq_head[:], in_=h_head[:], func=ACT.Square)
-        nc.vector.tensor_scalar(
-            out=slope[:, 0, :], in0=sq_head[:], scalar1=-1.0, scalar2=1.0, op0=ALU.mult, op1=ALU.add
-        )
+        slope = [sb.tile([P, N], F32, name="slope%d" % t) for t in range(2)]
+        late_slopes = []
+        sq = {}
 
-        u = []
-        u_banks = []
+        def square(t, tag):
+            sq[t] = sb.tile([P, N], F32, name="sq", tag=tag, align_bytes=64)
+            nc.scalar.activation(out=sq[t][:], in_=h_head[t][:], func=ACT.Square)
+
+        def affine(t):
+            nc.vector.tensor_scalar(out=slope[t][:], in0=sq[t][:], scalar1=-1.0, scalar2=1.0, op0=ALU.mult, op1=ALU.add)
+
+        square(0, "sq0")
+        square(1, "sq1")
+        affine(0)
+        quantise_wo(2, HALF, N)
+
+        banks_u = []
         for t in range(PACK):
-            bank = ps.tile([P, N], F32, name="u_bank%d" % t)
-            cols = slice(t * P, (t + 1) * P)
+            bank = ps.tile([P, N], F32, name="u_bank", tag="u_bank%d" % t)
             nc.tensor.matmul_mx(
                 out=bank[:],
-                lhsT=wo_codes[:, cols].bitcast(E4M3),
-                lhsT_scale=wo_scales[:, cols],
+                lhsT=wo_plane[t].bitcast(E4M3),
+                lhsT_scale=wo_scales[:, t * P : (t + 1) * P],
                 rhs=dy_codes[:].bitcast(E5M2),
                 rhs_scale=dy_scales[:],
                 start=True,
                 stop=True,
             )
-            u_t = sb.tile([P, 2 * N], F32, name="u%d" % t)
-            nc.vector.memset(u_t[:, N : 2 * N], 0.0)
-            nc.scalar.copy(out=u_t[:, 0:N], in_=bank[:])
-            u.append(u_t)
-            u_banks.append(bank)
+            banks_u.append(bank)
 
-        picked = sb.tile([P, PACK, N], F32, name="picked")
-        for t in range(PACK):
-            nc.vector.tensor_copy(out=picked[:, t, :], in_=u[t][:].indirect(offsets[:]))
+        u = [sb.tile([P, 2 * N], F32, name="u%d" % t) for t in range(2)]
+        for t in range(2):
+            nc.vector.memset(u[t][:, N : 2 * N], 0.0)
+        u.extend(sb.tile([P, N], F32, name="u%d" % t) for t in range(2, PACK))
+        dz = sb.tile([P, PACK, N], F32, name="dz")
 
-        sq_rest = sb.tile([P, PACK - 1, N], F32, name="sq_rest", tag="dy_codes", align_bytes=64)
-        nc.scalar.activation(out=sq_rest[:], in_=h_rest[:], func=ACT.Square)
+        def fetch(t):
+            nc.vector.tensor_tensor(out=dz[:, t, :], in0=u[t][:].indirect(offsets[:]), in1=slope[t][:], op=ALU.mult)
+
+        nc.scalar.copy(out=u[0][:, 0:N], in_=banks_u[0][:])
+        fetch(0)
+        nc.scalar.copy(out=u[1][:, 0:N], in_=banks_u[1][:])
+        nc.scalar.activation(out=slope[1][:], in_=sq[1][:], func=ACT.Identity, scale=-1.0, bias=1.0)
+        fetch(1)
         for a in range(2):
             tokens = slice(a * HALF, (a + 1) * HALF)
-            nc.scalar.activation(
-                out=slope[:, 1:PACK, tokens], in_=sq_rest[:, :, tokens], func=ACT.Identity, scale=-1.0, bias=1.0
+            nc.scalar.copy(out=u[2 + a][:], in_=banks_u[2 + a][:])
+            sq_late = sb.tile([P, 2, HALF], F32, name="sq_late", tag="wo_codes%d" % (1 + a), align_bytes=64)
+            nc.scalar.activation(out=sq_late[:], in_=h_rest[:, :, tokens], func=ACT.Square)
+            slope_late = sb.tile([P, 2, HALF], F32, name="slope_late%d" % a)
+            late_slopes.append((sq_late, slope_late))
+        for a in range(2):
+            tokens = slice(a * HALF, (a + 1) * HALF)
+            sq_late, slope_late = late_slopes[a]
+            nc.vector.tensor_scalar(
+                out=slope_late[:], in0=sq_late[:], scalar1=-1.0, scalar2=1.0, op0=ALU.mult, op1=ALU.add
+            )
+            for t in range(2):
+                nc.vector.tensor_tensor(
+                    out=dz[:, 2 + t, tokens],
+                    in0=u[2 + t][:].indirect(offsets[:, 16 * a : 16 * a + 16]),
+                    in1=slope_late[:, t, :],
+                    op=ALU.mult,
+                )
+
+        warm = ps.tile([P, N], F32, name="warm", tag="u_bank3")
+        for t in range(2):
+            nc.tensor.matmul_mx(
+                out=warm[:],
+                lhsT=wo_plane[0].bitcast(E4M3),
+                lhsT_scale=wo_scales[:, 0:P],
+                rhs=dy_codes[:].bitcast(E5M2),
+                rhs_scale=dy_scales[:],
+                start=True,
+                stop=True,
             )
 
         w_dst = w_bf[:].rearrange("p (t m j) -> p m j t", t=PACK, j=PACK)
         w_src = w_raw[:].rearrange("p j (m t) -> p m j t", t=PACK)
-        for t in (0, 2):
-            nc.scalar.activation(out=w_dst[:, :, :, t : t + 2], in_=w_src[:, :, :, t : t + 2], func=ACT.Copy)
 
-        def through_tanh(c0, c1):
-            nc.vector.tensor_tensor(
-                out=weave(dz_bf, c0, c1), in0=runs(picked, c0, c1), in1=runs(slope, c0, c1), op=ALU.mult
-            )
-
-        through_tanh(0, 192)
-        through_tanh(192, HALF)
-        quantise(nc, dz_codes, dz_scales, dz_bf, E5M2, 0, P)
-        for bank in u_banks[0:2]:
-            nc.tensor.matmul_mx(
-                out=bank[:],
-                lhsT=dz_codes[:, 0:P].bitcast(E5M2),
-                lhsT_scale=dz_scales[:, 0:P],
-                rhs=wo_codes[:].bitcast(E4M3),
-                rhs_scale=wo_scales[:],
-                start=True,
-                stop=True,
-            )
-        through_tanh(HALF, N)
-        quantise(nc, dz_codes, dz_scales, dz_bf, E5M2, P, HALF)
+        nc.scalar.activation(out=w_dst[:, :, :, 0:2], in_=w_src[:, :, :, 0:2], func=ACT.Copy)
+        nc.scalar.activation(out=weave(dz_bf, 0, HALF), in_=runs(dz, 0, HALF), func=ACT.Copy)
+        nc.scalar.activation(out=weave(dz_bf, HALF, 3 * P), in_=runs(dz, HALF, 3 * P), func=ACT.Copy)
+        nc.vector.tensor_copy(out=weave(dz_bf, 3 * P, N), in_=runs(dz, 3 * P, N))
         quantise(nc, w_codes, w_scales, w_bf, E4M3, 0, P)
+        quantise(nc, dz_codes, dz_scales, dz_bf, E5M2, 0, HALF)
         quantise(nc, dz_codes, dz_scales, dz_bf, E5M2, HALF, N)
-        quantise(nc, w_codes, w_scales, w_bf, E4M3, P, 2 * P)
-        quantise(nc, w_codes, w_scales, w_bf, E4M3, 2 * P, N)
+        quantise(nc, w_codes, w_scales, w_bf, E4M3, P, HALF)
+
+        half_m = P // 2
+        late = [
+            sb.tile([P, 2 * half_m * PACK], BF16, name="w_late", tag=tag, align_bytes=64) for tag in ("w_late", "dz_bf")
+        ]
+        for a in range(2):
+            dst = late[a][:].rearrange("p (t m j) -> p m j t", t=2, j=PACK)
+            src = w_src[:, a * half_m : (a + 1) * half_m, :, 2:4]
+            if a == 0:
+                nc.scalar.activation(out=dst, in_=src, func=ACT.Copy)
+            else:
+                nc.vector.tensor_copy(out=dst, in_=src)
+        for t in range(2):
+            for a in range(2):
+                c0 = (2 + t) * P + a * half_m
+                nc.vector.quantize_mx(
+                    out=w_codes[:, c0 : c0 + half_m].bitcast(E4M3),
+                    scales=w_scales[:, c0 : c0 + half_m],
+                    in_=late[a][:, t * half_m * PACK : (t + 1) * half_m * PACK],
+                )
 
         y_lo = sb.tile([P, 2, N], F32, name="y_lo")
         y_hi = sb.tile([P, 2, N], F32, name="y_hi")
@@ -172,7 +222,7 @@ def tile_attend_ghsort_tnh_pl_kernel(tc, wo, dyT, W, h, offs, out_0, out_1, out_
                 stop=True,
             )
             banks.append(bank)
-        nc.vector.tensor_copy(out=y_lo[:, 0, :], in_=banks[0][:])
+        nc.scalar.copy(out=y_lo[:, 0, :], in_=banks[0][:])
         nc.sync.dma_start(out=y_rows[:, 0, :], in_=y_lo[:, 0, :])
         nc.scalar.copy(out=y_lo[:, 1, :], in_=banks[1][:])
         nc.sync.dma_start(out=y_rows[:, 1, :], in_=y_lo[:, 1, :])

@@ -160,18 +160,6 @@ def tile_attend_ghsort_tnh_pl_kernel(tc, wo, dyT, W, h, offs, out_0, out_1, out_
                     op=ALU.mult,
                 )
 
-        warm = ps.tile([P, N], F32, name="warm", tag="u_bank3")
-        for t in range(2):
-            nc.tensor.matmul_mx(
-                out=warm[:],
-                lhsT=wo_plane[0].bitcast(E4M3),
-                lhsT_scale=wo_scales[:, 0:P],
-                rhs=dy_codes[:].bitcast(E5M2),
-                rhs_scale=dy_scales[:],
-                start=True,
-                stop=True,
-            )
-
         w_dst = w_bf[:].rearrange("p (t m j) -> p m j t", t=PACK, j=PACK)
         w_src = w_raw[:].rearrange("p j (m t) -> p m j t", t=PACK)
 
@@ -204,10 +192,8 @@ def tile_attend_ghsort_tnh_pl_kernel(tc, wo, dyT, W, h, offs, out_0, out_1, out_
                     in_=late[a][:, t * half_m * PACK : (t + 1) * half_m * PACK],
                 )
 
-        y_lo = sb.tile([P, 2, N], F32, name="y_lo")
-        y_hi = sb.tile([P, 2, N], F32, name="y_hi")
+        y = sb.tile([P, PACK, N], F32, name="y")
         y_rows = out_0.rearrange("(p t) c -> p t c", t=PACK)
-        y_words = y_bf[:].rearrange("p (c t) -> p c t", t=PACK)
         banks = []
         for t in range(PACK):
             bank = ps.tile([P, N], F32, name="y_bank%d" % t)
@@ -222,20 +208,17 @@ def tile_attend_ghsort_tnh_pl_kernel(tc, wo, dyT, W, h, offs, out_0, out_1, out_
                 stop=True,
             )
             banks.append(bank)
-        nc.scalar.copy(out=y_lo[:, 0, :], in_=banks[0][:])
-        nc.sync.dma_start(out=y_rows[:, 0, :], in_=y_lo[:, 0, :])
-        nc.scalar.copy(out=y_lo[:, 1, :], in_=banks[1][:])
-        nc.sync.dma_start(out=y_rows[:, 1, :], in_=y_lo[:, 1, :])
-        nc.vector.tensor_copy(out=y_words[:, :, 0:2], in_=y_lo[:].rearrange("p t c -> p c t"))
-        nc.scalar.copy(out=y_hi[:, 0, :], in_=banks[2][:])
-        nc.sync.dma_start(out=y_rows[:, 2, :], in_=y_hi[:, 0, :])
-        first, second, third = slice(0, 256), slice(256, 384), slice(384, 512)
-        for tokens in (first, third, second):
-            nc.scalar.copy(out=y_hi[:, 1, tokens], in_=banks[3][:, tokens])
-        for tokens in (first, second):
-            nc.vector.tensor_copy(out=y_words[:, tokens, 2:4], in_=y_hi[:, :, tokens].rearrange("p t c -> p c t"))
-        nc.scalar.copy(out=y_words[:, third, 2:4], in_=y_hi[:, :, third].rearrange("p t c -> p c t"))
-        nc.sync.dma_start(out=y_rows[:, 3, :], in_=y_hi[:, 1, :])
+        for t in range(PACK - 1):
+            copy = nc.vector.tensor_copy if t == 2 else nc.scalar.copy
+            copy(out=y[:, t, :], in_=banks[t][:])
+            nc.sync.dma_start(out=y_rows[:, t, :], in_=y[:, t, :])
+        ycut = 352
+        for c0, c1 in ((0, HALF), (ycut, N), (HALF, ycut)):
+            nc.scalar.copy(out=y[:, 3, c0:c1], in_=banks[3][:, c0:c1])
+        nc.vector.tensor_copy(out=weave(y_bf, 0, HALF), in_=runs(y, 0, HALF))
+        nc.vector.tensor_copy(out=weave(y_bf, HALF, ycut), in_=runs(y, HALF, ycut))
+        nc.scalar.copy(out=weave(y_bf, ycut, N), in_=runs(y, ycut, N))
+        nc.sync.dma_start(out=y_rows[:, 3, :], in_=y[:, 3, :])
         words = out_1.rearrange("g p c l -> (g p) (c l)").bitcast(I32)
         for a in range(2):
             quantise(nc, y_codes, y_scales, y_bf, E4M3, a * HALF, (a + 1) * HALF)

@@ -88,20 +88,20 @@ def tile_attend_ghsort_tnh_pl_kernel(tc, wo, dyT, W, h, offs, out_0, out_1, out_
 
         wo_dst = wo_bf[:].rearrange("p (t m j) -> p m j t", t=PACK, j=PACK)
         wo_src = wo_raw[:].rearrange("p j (m t) -> p m j t", t=PACK)
-        mcut = 92
+        mcut = 76
         nc.vector.tensor_copy(out=wo_dst[:, 0:mcut, :, 0:2], in_=wo_src[:, 0:mcut, :, 0:2])
         nc.scalar.activation(out=wo_dst[:, mcut:P, :, 0:2], in_=wo_src[:, mcut:P, :, 0:2], func=ACT.Copy)
         quantise_wo(0, 0, P)
         quantise_wo(1, P, HALF)
         nc.vector.tensor_copy(out=wo_dst[:, :, :, 2:4], in_=wo_src[:, :, :, 2:4])
 
-        slope = [sb.tile([P, N], F32, name="slope%d" % t) for t in range(2)]
-        late_slopes = []
+        slope = [sb.tile([P, N], F32, name="slope%d" % t) for t in range(PACK)]
+        h_lane = [h_head[0][:], h_head[1][:], h_rest[:, 0, :], h_rest[:, 1, :]]
         sq = {}
 
         def square(t, tag):
             sq[t] = sb.tile([P, N], F32, name="sq", tag=tag, align_bytes=64)
-            nc.scalar.activation(out=sq[t][:], in_=h_head[t][:], func=ACT.Square)
+            nc.scalar.activation(out=sq[t][:], in_=h_lane[t], func=ACT.Square)
 
         def affine(t):
             nc.vector.tensor_scalar(out=slope[t][:], in0=sq[t][:], scalar1=-1.0, scalar2=1.0, op0=ALU.mult, op1=ALU.add)
@@ -110,6 +110,7 @@ def tile_attend_ghsort_tnh_pl_kernel(tc, wo, dyT, W, h, offs, out_0, out_1, out_
         square(1, "sq1")
         affine(0)
         quantise_wo(2, HALF, N)
+        affine(1)
 
         banks_u = []
         for t in range(PACK):
@@ -125,48 +126,42 @@ def tile_attend_ghsort_tnh_pl_kernel(tc, wo, dyT, W, h, offs, out_0, out_1, out_
             )
             banks_u.append(bank)
 
-        u = [sb.tile([P, 2 * N], F32, name="u%d" % t) for t in range(2)]
-        for t in range(2):
+        u = [sb.tile([P, 2 * N], F32, name="u%d" % t) for t in range(PACK - 1)]
+        for t in range(PACK - 1):
             nc.vector.memset(u[t][:, N : 2 * N], 0.0)
-        u.extend(sb.tile([P, N], F32, name="u%d" % t) for t in range(2, PACK))
+        u.append(sb.tile([P, N], F32, name="u3"))
         dz = sb.tile([P, PACK, N], F32, name="dz")
 
         def fetch(t):
             nc.vector.tensor_tensor(out=dz[:, t, :], in0=u[t][:].indirect(offsets[:]), in1=slope[t][:], op=ALU.mult)
 
-        nc.scalar.copy(out=u[0][:, 0:N], in_=banks_u[0][:])
-        fetch(0)
-        nc.scalar.copy(out=u[1][:, 0:N], in_=banks_u[1][:])
-        nc.scalar.activation(out=slope[1][:], in_=sq[1][:], func=ACT.Identity, scale=-1.0, bias=1.0)
-        fetch(1)
+        for t in range(2):
+            nc.scalar.copy(out=u[t][:, 0:N], in_=banks_u[t][:])
+            fetch(t)
+        square(2, "wo_codes0")
+        square(3, "wo_codes1")
+        nc.scalar.activation(out=slope[2][:], in_=sq[2][:], func=ACT.Identity, scale=-1.0, bias=1.0)
+        affine(3)
+        for t in range(2, PACK):
+            nc.scalar.copy(out=u[t][:, 0:N], in_=banks_u[t][:])
+        fetch(2)
         for a in range(2):
             tokens = slice(a * HALF, (a + 1) * HALF)
-            nc.scalar.copy(out=u[2 + a][:], in_=banks_u[2 + a][:])
-            sq_late = sb.tile([P, 2, HALF], F32, name="sq_late", tag="wo_codes%d" % (1 + a), align_bytes=64)
-            nc.scalar.activation(out=sq_late[:], in_=h_rest[:, :, tokens], func=ACT.Square)
-            slope_late = sb.tile([P, 2, HALF], F32, name="slope_late%d" % a)
-            late_slopes.append((sq_late, slope_late))
-        for a in range(2):
-            tokens = slice(a * HALF, (a + 1) * HALF)
-            sq_late, slope_late = late_slopes[a]
-            nc.vector.tensor_scalar(
-                out=slope_late[:], in0=sq_late[:], scalar1=-1.0, scalar2=1.0, op0=ALU.mult, op1=ALU.add
+            nc.vector.tensor_tensor(
+                out=dz[:, 3, tokens],
+                in0=u[3][:].indirect(offsets[:, 16 * a : 16 * a + 16]),
+                in1=slope[3][:, tokens],
+                op=ALU.mult,
             )
-            for t in range(2):
-                nc.vector.tensor_tensor(
-                    out=dz[:, 2 + t, tokens],
-                    in0=u[2 + t][:].indirect(offsets[:, 16 * a : 16 * a + 16]),
-                    in1=slope_late[:, t, :],
-                    op=ALU.mult,
-                )
 
+        zcut = 352
         w_dst = w_bf[:].rearrange("p (t m j) -> p m j t", t=PACK, j=PACK)
         w_src = w_raw[:].rearrange("p j (m t) -> p m j t", t=PACK)
 
         nc.scalar.activation(out=w_dst[:, :, :, 0:2], in_=w_src[:, :, :, 0:2], func=ACT.Copy)
         nc.scalar.activation(out=weave(dz_bf, 0, HALF), in_=runs(dz, 0, HALF), func=ACT.Copy)
-        nc.scalar.activation(out=weave(dz_bf, HALF, 3 * P), in_=runs(dz, HALF, 3 * P), func=ACT.Copy)
-        nc.vector.tensor_copy(out=weave(dz_bf, 3 * P, N), in_=runs(dz, 3 * P, N))
+        nc.scalar.activation(out=weave(dz_bf, HALF, zcut), in_=runs(dz, HALF, zcut), func=ACT.Copy)
+        nc.vector.tensor_copy(out=weave(dz_bf, zcut, N), in_=runs(dz, zcut, N))
         quantise(nc, w_codes, w_scales, w_bf, E4M3, 0, P)
         quantise(nc, dz_codes, dz_scales, dz_bf, E5M2, 0, HALF)
         quantise(nc, dz_codes, dz_scales, dz_bf, E5M2, HALF, N)

@@ -154,17 +154,15 @@ def tile_attend_ghsort_tnh_pl_kernel(tc, wo, dyT, W, h, offs, out_0, out_1, out_
                 op=ALU.mult,
             )
 
-        zcut = 352
         w_dst = w_bf[:].rearrange("p (t m j) -> p m j t", t=PACK, j=PACK)
         w_src = w_raw[:].rearrange("p j (m t) -> p m j t", t=PACK)
 
         nc.scalar.activation(out=w_dst[:, :, :, 0:2], in_=w_src[:, :, :, 0:2], func=ACT.Copy)
         nc.scalar.activation(out=weave(dz_bf, 0, HALF), in_=runs(dz, 0, HALF), func=ACT.Copy)
-        nc.scalar.activation(out=weave(dz_bf, HALF, zcut), in_=runs(dz, HALF, zcut), func=ACT.Copy)
-        nc.vector.tensor_copy(out=weave(dz_bf, zcut, N), in_=runs(dz, zcut, N))
+        nc.vector.tensor_copy(out=weave(dz_bf, HALF, N), in_=runs(dz, HALF, N))
         quantise(nc, w_codes, w_scales, w_bf, E4M3, 0, P)
-        quantise(nc, dz_codes, dz_scales, dz_bf, E5M2, 0, HALF)
         quantise(nc, dz_codes, dz_scales, dz_bf, E5M2, HALF, N)
+        quantise(nc, dz_codes, dz_scales, dz_bf, E5M2, 0, HALF)
         quantise(nc, w_codes, w_scales, w_bf, E4M3, P, HALF)
 
         half_m = P // 2

@@ -64,9 +64,12 @@ def tile_attend_ghsort_tnh_pl_kernel(tc, wo, dyT, W, h, offs, out_0, out_1, out_
             scales = sb.tile([P, N], U8, name=name + "_scales", tag=name + "_scales", align_bytes=64)
             return grouped, codes, scales
 
-        dy_bf, dy_codes, dy_scales = operand("dy")
-        w_bf, w_codes, w_scales = operand("w")
-        dz_bf, dz_codes, dz_scales = operand("dz")
+        w_codes = sb.tile([P, N], U32, name="w_codes", align_bytes=64)
+        w_scales = sb.tile([P, N], U8, name="w_scales", align_bytes=64)
+        w_bf = sb.tile([P, 2 * P * PACK], BF16, name="w_bf", tag="w_bf", align_bytes=64)
+        dy_bf = sb.tile([P, N * PACK], BF16, name="dy_bf", align_bytes=64)
+        grad_codes = sb.tile([P, 2 * N], U32, name="grad_codes", align_bytes=64)
+        grad_scales = sb.tile([P, 2 * N], U8, name="grad_scales", align_bytes=64)
         y_bf, y_codes, y_scales = operand("y")
         wo_bf = sb.tile([P, N * PACK], BF16, name="wo_bf", align_bytes=64)
         wo_scales = sb.tile([P, N], U8, name="wo_scales", align_bytes=64)
@@ -79,7 +82,7 @@ def tile_attend_ghsort_tnh_pl_kernel(tc, wo, dyT, W, h, offs, out_0, out_1, out_
         cut = 320
         nc.vector.tensor_copy(out=weave(dy_bf, 0, cut), in_=runs(dy_raw, 0, cut))
         nc.scalar.activation(out=weave(dy_bf, cut, N), in_=runs(dy_raw, cut, N), func=ACT.Copy)
-        quantise(nc, dy_codes, dy_scales, dy_bf, E5M2, 0, N)
+        quantise(nc, grad_codes, grad_scales, dy_bf, E5M2, 0, N)
 
         def quantise_wo(a, c0, c1):
             nc.vector.quantize_mx(
@@ -103,71 +106,105 @@ def tile_attend_ghsort_tnh_pl_kernel(tc, wo, dyT, W, h, offs, out_0, out_1, out_
             sq[t] = sb.tile([P, N], F32, name="sq", tag=tag, align_bytes=64)
             nc.scalar.activation(out=sq[t][:], in_=h_lane[t], func=ACT.Square)
 
-        def affine(t):
-            nc.vector.tensor_scalar(out=slope[t][:], in0=sq[t][:], scalar1=-1.0, scalar2=1.0, op0=ALU.mult, op1=ALU.add)
+        def affine(out, squares):
+            nc.vector.tensor_scalar(out=out, in0=squares, scalar1=-1.0, scalar2=1.0, op0=ALU.mult, op1=ALU.add)
 
         square(0, "sq0")
         square(1, "sq1")
-        affine(0)
+        affine(slope[0][:], sq[0][:])
         quantise_wo(2, HALF, N)
-        affine(1)
+        affine(slope[1][:], sq[1][:])
 
-        banks_u = []
-        for t in range(PACK):
-            bank = ps.tile([P, N], F32, name="u_bank", tag="u_bank%d" % t)
+        def product(tag, codes, scales, c0):
+            bank = ps.tile([P, N], F32, name="bank", tag=tag)
             nc.tensor.matmul_mx(
                 out=bank[:],
-                lhsT=wo_plane[t].bitcast(E4M3),
-                lhsT_scale=wo_scales[:, t * P : (t + 1) * P],
-                rhs=dy_codes[:].bitcast(E5M2),
-                rhs_scale=dy_scales[:],
+                lhsT=codes.bitcast(E4M3),
+                lhsT_scale=scales,
+                rhs=grad_codes[:, c0 : c0 + N].bitcast(E5M2),
+                rhs_scale=grad_scales[:, c0 : c0 + N],
                 start=True,
                 stop=True,
             )
-            banks_u.append(bank)
+            return bank
 
-        u = [sb.tile([P, 2 * N], F32, name="u%d" % t) for t in range(PACK - 1)]
-        for t in range(PACK - 1):
+        banks_u = [product("bank%d" % t, wo_plane[t], wo_scales[:, t * P : (t + 1) * P], 0) for t in range(PACK)]
+
+        u = [sb.tile([P, 2 * N], F32, name="u%d" % t) for t in range(2)]
+        for t in range(2):
             nc.vector.memset(u[t][:, N : 2 * N], 0.0)
-        u.append(sb.tile([P, N], F32, name="u3"))
-        dz = sb.tile([P, PACK, N], F32, name="dz")
+        u.append(sb.tile([P, N], F32, name="u2"))
+        u.append(sb.tile([P, N], F32, name="u3", tag="u3", align_bytes=64))
+        dz = sb.tile([P, 7 * N], F32, name="dz")
+
+        def dz_at(t, c0, c1):
+            first = t * N + (3 * HALF if t >= 2 and c0 >= HALF else 0)
+            return dz[:, first + c0 : first + c1]
+
 
         def fetch(t):
-            nc.vector.tensor_tensor(out=dz[:, t, :], in0=u[t][:].indirect(offsets[:]), in1=slope[t][:], op=ALU.mult)
+            nc.vector.tensor_tensor(out=dz_at(t, 0, N), in0=u[t][:].indirect(offsets[:]), in1=slope[t][:], op=ALU.mult)
 
         for t in range(2):
             nc.scalar.copy(out=u[t][:, 0:N], in_=banks_u[t][:])
             fetch(t)
         square(2, "wo_codes0")
         square(3, "wo_codes1")
-        nc.scalar.activation(out=slope[2][:], in_=sq[2][:], func=ACT.Identity, scale=-1.0, bias=1.0)
-        affine(3)
+
+        def affine_scalar(c0, c1):
+            nc.scalar.activation(out=slope[2][:, c0:c1], in_=sq[2][:, c0:c1], func=ACT.Identity, scale=-1.0, bias=1.0)
+
+        affine_scalar(0, HALF)
+        affine(slope[3][:], sq[3][:])
         for t in range(2, PACK):
             nc.scalar.copy(out=u[t][:, 0:N], in_=banks_u[t][:])
-        fetch(2)
-        for a in range(2):
-            tokens = slice(a * HALF, (a + 1) * HALF)
+        affine_scalar(HALF, N)
+
+        def fetch_part(t, c0, c1):
             nc.vector.tensor_tensor(
-                out=dz[:, 3, tokens],
-                in0=u[3][:].indirect(offsets[:, 16 * a : 16 * a + 16]),
-                in1=slope[3][:, tokens],
+                out=dz_at(t, c0, c1),
+                in0=u[t][:].indirect(offsets[:, c0 // 16 : c1 // 16]),
+                in1=slope[t][:, c0:c1],
                 op=ALU.mult,
             )
 
-        w_dst = w_bf[:].rearrange("p (t m j) -> p m j t", t=PACK, j=PACK)
-        w_src = w_raw[:].rearrange("p j (m t) -> p m j t", t=PACK)
+        def weave_dz(copy, tile, first, c0, c1):
+            span = 2 * N + (3 * HALF if c0 >= HALF else 0)
+            pairs = dz[:, 0 : 2 * span].rearrange("p (a s) -> p a s", a=2)
+            lanes = pairs[:, :, 0 : 2 * N].rearrange("p a (b c) -> p a b c", b=2)[:, :, :, c0:c1]
+            copy(
+                out=tile[:, (c0 - first) * PACK : (c1 - first) * PACK].rearrange("p (c i a b) -> p c a b i", i=4, a=2, b=2),
+                in_=lanes.rearrange("p a b (c i) -> p c a b i", i=4),
+            )
 
-        nc.scalar.activation(out=w_dst[:, :, :, 0:2], in_=w_src[:, :, :, 0:2], func=ACT.Copy)
-        nc.scalar.activation(out=weave(dz_bf, 0, HALF), in_=runs(dz, 0, HALF), func=ACT.Copy)
-        nc.vector.tensor_copy(out=weave(dz_bf, HALF, N), in_=runs(dz, HALF, N))
-        quantise(nc, w_codes, w_scales, w_bf, E4M3, 0, P)
-        quantise(nc, dz_codes, dz_scales, dz_bf, E5M2, HALF, N)
-        quantise(nc, dz_codes, dz_scales, dz_bf, E5M2, 0, HALF)
-        quantise(nc, w_codes, w_scales, w_bf, E4M3, P, HALF)
+        def product_w(tag, t, c0):
+            return product(tag, w_codes[:, t * P : (t + 1) * P], w_scales[:, t * P : (t + 1) * P], c0)
+
+        for a in range(2):
+            for t in range(2, PACK):
+                fetch_part(t, a * HALF, (a + 1) * HALF)
+        w_dst = w_bf[:].rearrange("p (t m j) -> p m j t", t=2, j=PACK)
+        w_src = w_raw[:].rearrange("p j (m t) -> p m j t", t=PACK)
+        dz_bf = [sb.tile([P, P * PACK], BF16, name="dz_bf", tag="dz_bf%d" % k, align_bytes=64) for k in range(2)]
+        wcut = 80
+        nc.scalar.activation(out=w_dst[:, 0:wcut], in_=w_src[:, 0:wcut, :, 0:2], func=ACT.Copy)
+        weave_dz(nc.scalar.copy, dz_bf[0], 0, 0, P)
+        nc.scalar.activation(out=w_dst[:, wcut:P], in_=w_src[:, wcut:P, :, 0:2], func=ACT.Copy)
+        weave_dz(nc.scalar.copy, dz_bf[1], P, P, HALF)
+        quantise(nc, grad_codes, grad_scales, dz_bf[0], E5M2, 0, P, shift=N)
+        for t in range(2):
+            quantise(nc, w_codes, w_scales, w_bf, E4M3, t * P, (t + 1) * P)
+        early = [product_w("early%d" % t, t, P) for t in range(2)]
+        dz_rest = sb.tile([P, HALF * PACK], BF16, name="dz_rest", tag="dz_bf0", align_bytes=64)
+        zcut = 416
+        weave_dz(nc.vector.tensor_copy, dz_rest, HALF, HALF, zcut)
+        weave_dz(nc.scalar.copy, dz_rest, HALF, zcut, N)
+        quantise(nc, grad_codes, grad_scales, dz_bf[1], E5M2, 0, P, shift=N + P)
+        quantise(nc, grad_codes, grad_scales, dz_rest, E5M2, 0, HALF, shift=N + HALF)
 
         half_m = P // 2
         late = [
-            sb.tile([P, 2 * half_m * PACK], BF16, name="w_late", tag=tag, align_bytes=64) for tag in ("w_late", "dz_bf")
+            sb.tile([P, 2 * half_m * PACK], BF16, name="w_late", tag=tag, align_bytes=64) for tag in ("w_bf", "dz_bf1")
         ]
         for a in range(2):
             dst = late[a][:].rearrange("p (t m j) -> p m j t", t=2, j=PACK)
@@ -186,25 +223,18 @@ def tile_attend_ghsort_tnh_pl_kernel(tc, wo, dyT, W, h, offs, out_0, out_1, out_
                 )
 
         y = sb.tile([P, PACK, N], F32, name="y")
+        y_first = y[:, 0:2, 0:P]
         y_rows = out_0.rearrange("(p t) c -> p t c", t=PACK)
-        banks = []
-        for t in range(PACK):
-            bank = ps.tile([P, N], F32, name="y_bank%d" % t)
-            cols = slice(t * P, (t + 1) * P)
-            nc.tensor.matmul_mx(
-                out=bank[:],
-                lhsT=w_codes[:, cols].bitcast(E4M3),
-                lhsT_scale=w_scales[:, cols],
-                rhs=dz_codes[:].bitcast(E5M2),
-                rhs_scale=dz_scales[:],
-                start=True,
-                stop=True,
-            )
-            banks.append(bank)
-        for t in range(PACK - 1):
-            copy = nc.vector.tensor_copy if t == 2 else nc.scalar.copy
-            copy(out=y[:, t, :], in_=banks[t][:])
-            nc.sync.dma_start(out=y_rows[:, t, :], in_=y[:, t, :])
+        for t in range(2):
+            nc.scalar.copy(out=y_first[:, t, :], in_=early[t][:, N - P : N])
+        nc.sync.dma_start(out=y_rows[:, 0:2, 0:P], in_=y_first)
+        banks = [product_w("bank%d" % t, t, N) for t in range(PACK)]
+        for t, copy in enumerate((nc.scalar.copy, nc.vector.tensor_copy)):
+            copy(out=y[:, t, P:N], in_=banks[t][:, P:N])
+            nc.sync.dma_start(out=y_rows[:, t, P:N], in_=y[:, t, P:N])
+        for a in range(2):
+            nc.vector.tensor_copy(out=y[:, 2, a * HALF : (a + 1) * HALF], in_=banks[2][:, a * HALF : (a + 1) * HALF])
+        nc.sync.dma_start(out=y_rows[:, 2, :], in_=y[:, 2, :])
         ycut = 352
         for c0, c1 in ((0, HALF), (ycut, N), (HALF, ycut)):
             nc.scalar.copy(out=y[:, 3, c0:c1], in_=banks[3][:, c0:c1])

@@ -45,17 +45,17 @@ def tile_attend_ghsort_tnh_pl_kernel(tc, wo, dyT, W, h, offs, out_0, out_1, out_
         offsets = sb.tile([P, N // 16], U16, name="offsets")
         wo_raw = sb.tile([P, PACK, N], F32, name="wo_raw")
         dy_raw = sb.tile([P, PACK, N], F32, name="dy_raw")
-        h_head = [sb.tile([P, N], F32, name="h_head%d" % j) for j in range(2)]
-        h_rest = sb.tile([P, 2, N], F32, name="h_rest")
+        h_cuts = (0, 640, 1280, PACK * N)
+        h_part = [sb.tile([P, h_cuts[a + 1] - h_cuts[a]], F32, name="h_part%d" % a) for a in range(3)]
         w_raw = sb.tile([P, PACK, N], F32, name="w_raw")
 
-        h_rows = h.rearrange("(p j) c -> p j c", j=PACK)
+        h_rows = h.rearrange("(p j) c -> p (j c)", j=PACK)
         nc.sync.dma_start(out=dy_raw[:], in_=dyT.rearrange("(p j) c -> p j c", j=PACK))
         nc.sync.dma_start(out=wo_raw[:], in_=wo.rearrange("(p j) c -> p j c", j=PACK))
-        for j in range(2):
-            nc.sync.dma_start(out=h_head[j][:], in_=h_rows[:, j, :])
+        for a in range(2):
+            nc.sync.dma_start(out=h_part[a][:], in_=h_rows[:, h_cuts[a] : h_cuts[a + 1]])
         nc.sync.dma_start(offsets[:], offs)
-        nc.sync.dma_start(out=h_rest[:], in_=h_rows[:, 2:PACK, :])
+        nc.sync.dma_start(out=h_part[2][:], in_=h_rows[:, h_cuts[2] : h_cuts[3]])
         nc.sync.dma_start(out=w_raw[:], in_=W.rearrange("(p j) c -> p j c", j=PACK))
 
         def operand(name):
@@ -98,22 +98,21 @@ def tile_attend_ghsort_tnh_pl_kernel(tc, wo, dyT, W, h, offs, out_0, out_1, out_
         quantise_wo(1, P, HALF)
         nc.vector.tensor_copy(out=wo_dst[:, :, :, 2:4], in_=wo_src[:, :, :, 2:4])
 
-        slope = [sb.tile([P, N], F32, name="slope%d" % t) for t in range(PACK)]
-        h_lane = [h_head[0][:], h_head[1][:], h_rest[:, 0, :], h_rest[:, 1, :]]
-        sq = {}
+        slopes = sb.tile([P, PACK * N], F32, name="slopes", align_bytes=64)
+        slope = [slopes[:, t * N : (t + 1) * N] for t in range(PACK)]
 
-        def square(t, tag):
-            sq[t] = sb.tile([P, N], F32, name="sq", tag=tag, align_bytes=64)
-            nc.scalar.activation(out=sq[t][:], in_=h_lane[t], func=ACT.Square)
+        def square(source, width, tag):
+            sq = sb.tile([P, width], F32, name="sq", tag=tag, align_bytes=64)
+            nc.scalar.activation(out=sq[:], in_=source, func=ACT.Square)
+            return sq
 
         def affine(out, squares):
             nc.vector.tensor_scalar(out=out, in0=squares, scalar1=-1.0, scalar2=1.0, op0=ALU.mult, op1=ALU.add)
 
-        square(0, "sq0")
-        square(1, "sq1")
-        affine(slope[0][:], sq[0][:])
+        sq_head = [square(h_part[a][:], h_cuts[1], "sq%d" % a) for a in range(2)]
+        affine(slopes[:, 0 : h_cuts[1]], sq_head[0][:])
         quantise_wo(2, HALF, N)
-        affine(slope[1][:], sq[1][:])
+        affine(slopes[:, h_cuts[1] : h_cuts[2]], sq_head[1][:])
 
         def product(tag, codes, scales, c0):
             bank = ps.tile([P, N], F32, name="bank", tag=tag)
@@ -143,22 +142,27 @@ def tile_attend_ghsort_tnh_pl_kernel(tc, wo, dyT, W, h, offs, out_0, out_1, out_
 
 
         def fetch(t):
-            nc.vector.tensor_tensor(out=dz_at(t, 0, N), in0=u[t][:].indirect(offsets[:]), in1=slope[t][:], op=ALU.mult)
+            nc.vector.tensor_tensor(out=dz_at(t, 0, N), in0=u[t][:].indirect(offsets[:]), in1=slope[t], op=ALU.mult)
 
         for t in range(2):
             nc.scalar.copy(out=u[t][:, 0:N], in_=banks_u[t][:])
             fetch(t)
-        square(2, "wo_codes0")
-        square(3, "wo_codes1")
+        sq_late = square(h_part[2][:], 3 * HALF, "wo_codes1")
 
-        def affine_scalar(c0, c1):
-            nc.scalar.activation(out=slope[2][:, c0:c1], in_=sq[2][:, c0:c1], func=ACT.Identity, scale=-1.0, bias=1.0)
+        def affine_scalar(k):
+            nc.scalar.activation(
+                out=slopes[:, h_cuts[2] + k * HALF : h_cuts[2] + (k + 1) * HALF],
+                in_=sq_late[:, k * HALF : (k + 1) * HALF],
+                func=ACT.Identity,
+                scale=-1.0,
+                bias=1.0,
+            )
 
-        affine_scalar(0, HALF)
-        affine(slope[3][:], sq[3][:])
-        for t in range(2, PACK):
-            nc.scalar.copy(out=u[t][:, 0:N], in_=banks_u[t][:])
-        affine_scalar(HALF, N)
+        nc.scalar.copy(out=u[2][:], in_=banks_u[2][:])
+        affine_scalar(1)
+        nc.scalar.copy(out=u[3][:], in_=banks_u[3][:])
+        affine_scalar(0)
+        affine_scalar(2)
 
         def fetch_part(t, c0, c1):
             nc.vector.tensor_tensor(
@@ -195,32 +199,18 @@ def tile_attend_ghsort_tnh_pl_kernel(tc, wo, dyT, W, h, offs, out_0, out_1, out_
         for t in range(2):
             quantise(nc, w_codes, w_scales, w_bf, E4M3, t * P, (t + 1) * P)
         early = [product_w("early%d" % t, t, P) for t in range(2)]
-        dz_rest = sb.tile([P, HALF * PACK], BF16, name="dz_rest", tag="dz_bf0", align_bytes=64)
-        zcut = 416
-        weave_dz(nc.vector.tensor_copy, dz_rest, HALF, HALF, zcut)
-        weave_dz(nc.scalar.copy, dz_rest, HALF, zcut, N)
         quantise(nc, grad_codes, grad_scales, dz_bf[1], E5M2, 0, P, shift=N + P)
-        quantise(nc, grad_codes, grad_scales, dz_rest, E5M2, 0, HALF, shift=N + HALF)
+        dz_rest = sb.tile([P, HALF * PACK], BF16, name="dz_rest", tag="w_bf", align_bytes=64)
+        for c0 in (HALF, HALF + P):
+            weave_dz(nc.vector.tensor_copy, dz_rest, HALF, c0, c0 + P)
+        for c0 in (0, P):
+            quantise(nc, grad_codes, grad_scales, dz_rest, E5M2, c0, c0 + P, shift=N + HALF)
 
-        half_m = P // 2
-        late = [
-            sb.tile([P, 2 * half_m * PACK], BF16, name="w_late", tag=tag, align_bytes=64) for tag in ("w_bf", "dz_bf1")
-        ]
-        for a in range(2):
-            dst = late[a][:].rearrange("p (t m j) -> p m j t", t=2, j=PACK)
-            src = w_src[:, a * half_m : (a + 1) * half_m, :, 2:4]
-            if a == 0:
-                nc.scalar.activation(out=dst, in_=src, func=ACT.Copy)
-            else:
-                nc.vector.tensor_copy(out=dst, in_=src)
-        for t in range(2):
-            for a in range(2):
-                c0 = (2 + t) * P + a * half_m
-                nc.vector.quantize_mx(
-                    out=w_codes[:, c0 : c0 + half_m].bitcast(E4M3),
-                    scales=w_scales[:, c0 : c0 + half_m],
-                    in_=late[a][:, t * half_m * PACK : (t + 1) * half_m * PACK],
-                )
+        w_late = sb.tile([P, HALF * PACK], BF16, name="w_late", tag="dz_bf0", align_bytes=64)
+        nc.scalar.activation(
+            out=w_late[:].rearrange("p (t m j) -> p m j t", t=2, j=PACK), in_=w_src[:, :, :, 2:4], func=ACT.Copy
+        )
+        quantise(nc, w_codes, w_scales, w_late, E4M3, 0, HALF, shift=HALF)
 
         y = sb.tile([P, PACK, N], F32, name="y")
         y_first = y[:, 0:2, 0:P]

@@ -181,8 +181,16 @@ def tile_attend_ghsort_tnh_pl_kernel(tc, wo, dyT, W, h, offs, out_0, out_1, out_
                 in_=lanes.rearrange("p a b (c i) -> p c a b i", i=4),
             )
 
-        def product_w(tag, t, c0):
-            return product(tag, w_codes[:, t * P : (t + 1) * P], w_scales[:, t * P : (t + 1) * P], c0)
+        def product_w(out, t, c0, c1):
+            nc.tensor.matmul_mx(
+                out=out,
+                lhsT=w_codes[:, t * P : (t + 1) * P].bitcast(E4M3),
+                lhsT_scale=w_scales[:, t * P : (t + 1) * P],
+                rhs=grad_codes[:, N + c0 : N + c1].bitcast(E5M2),
+                rhs_scale=grad_scales[:, N + c0 : N + c1],
+                start=True,
+                stop=True,
+            )
 
         for a in range(2):
             for t in range(2, PACK):
@@ -198,7 +206,6 @@ def tile_attend_ghsort_tnh_pl_kernel(tc, wo, dyT, W, h, offs, out_0, out_1, out_
         quantise(nc, grad_codes, grad_scales, dz_bf[0], E5M2, 0, P, shift=N)
         for t in range(2):
             quantise(nc, w_codes, w_scales, w_bf, E4M3, t * P, (t + 1) * P)
-        early = [product_w("early%d" % t, t, P) for t in range(2)]
         quantise(nc, grad_codes, grad_scales, dz_bf[1], E5M2, 0, P, shift=N + P)
         dz_rest = sb.tile([P, HALF * PACK], BF16, name="dz_rest", tag="w_bf", align_bytes=64)
         for c0 in (HALF, HALF + P):
@@ -212,26 +219,35 @@ def tile_attend_ghsort_tnh_pl_kernel(tc, wo, dyT, W, h, offs, out_0, out_1, out_
         )
         quantise(nc, w_codes, w_scales, w_late, E4M3, 0, HALF, shift=HALF)
 
-        y = sb.tile([P, PACK, N], F32, name="y")
-        y_first = y[:, 0:2, 0:P]
+        y = [sb.tile([P, PACK, HALF], F32, name="y%d" % a) for a in range(2)]
         y_rows = out_0.rearrange("(p t) c -> p t c", t=PACK)
-        for t in range(2):
-            nc.scalar.copy(out=y_first[:, t, :], in_=early[t][:, N - P : N])
-        nc.sync.dma_start(out=y_rows[:, 0:2, 0:P], in_=y_first)
-        banks = [product_w("bank%d" % t, t, N) for t in range(PACK)]
-        for t, copy in enumerate((nc.scalar.copy, nc.vector.tensor_copy)):
-            copy(out=y[:, t, P:N], in_=banks[t][:, P:N])
-            nc.sync.dma_start(out=y_rows[:, t, P:N], in_=y[:, t, P:N])
-        for a in range(2):
-            nc.vector.tensor_copy(out=y[:, 2, a * HALF : (a + 1) * HALF], in_=banks[2][:, a * HALF : (a + 1) * HALF])
-        nc.sync.dma_start(out=y_rows[:, 2, :], in_=y[:, 2, :])
-        ycut = 352
-        for c0, c1 in ((0, HALF), (ycut, N), (HALF, ycut)):
-            nc.scalar.copy(out=y[:, 3, c0:c1], in_=banks[3][:, c0:c1])
-        nc.vector.tensor_copy(out=weave(y_bf, 0, HALF), in_=runs(y, 0, HALF))
-        nc.vector.tensor_copy(out=weave(y_bf, HALF, ycut), in_=runs(y, HALF, ycut))
-        nc.scalar.copy(out=weave(y_bf, ycut, N), in_=runs(y, ycut, N))
-        nc.sync.dma_start(out=y_rows[:, 3, :], in_=y[:, 3, :])
+
+        def planes(tag, a, t0, t1, copy):
+            bank = ps.tile([P, t1 - t0, HALF], F32, name="bank", tag=tag)
+            for t in range(t0, t1):
+                product_w(bank[:, t - t0, :], t, a * HALF, (a + 1) * HALF)
+            copy(out=y[a][:, t0:t1, :], in_=bank[:])
+
+        def store(a, t0, t1):
+            nc.sync.dma_start(out=y_rows[:, t0:t1, a * HALF : (a + 1) * HALF], in_=y[a][:, t0:t1, :])
+
+        def weave_y(copy, a, c0, c1):
+            copy(out=weave(y_bf, a * HALF + c0, a * HALF + c1), in_=runs(y[a], c0, c1))
+
+        planes("early0", 0, 0, 2, nc.scalar.copy)
+        store(0, 0, 2)
+        planes("early1", 1, 0, 2, nc.vector.tensor_copy)
+        store(1, 0, 2)
+        planes("bank0", 0, 2, 3, nc.scalar.copy)
+        planes("bank1", 0, 3, 4, nc.scalar.copy)
+        store(0, 2, 4)
+        planes("bank2", 1, 2, 3, nc.scalar.copy)
+        planes("bank3", 1, 3, 4, nc.scalar.copy)
+        store(1, 2, 4)
+        ycut = 160
+        weave_y(nc.vector.tensor_copy, 0, 0, HALF)
+        weave_y(nc.vector.tensor_copy, 1, 0, ycut)
+        weave_y(nc.scalar.copy, 1, ycut, HALF)
         words = out_1.rearrange("g p c l -> (g p) (c l)").bitcast(I32)
         for a in range(2):
             quantise(nc, y_codes, y_scales, y_bf, E4M3, a * HALF, (a + 1) * HALF)

@@ -197,27 +197,24 @@ def tile_attend_ghsort_tnh_pl_kernel(tc, wo, dyT, W, h, offs, out_0, out_1, out_
                 fetch_part(t, a * HALF, (a + 1) * HALF)
         w_dst = w_bf[:].rearrange("p (t m j) -> p m j t", t=2, j=PACK)
         w_src = w_raw[:].rearrange("p j (m t) -> p m j t", t=PACK)
-        dz_bf = [sb.tile([P, P * PACK], BF16, name="dz_bf", tag="dz_bf%d" % k, align_bytes=64) for k in range(2)]
-        wcut = 80
+        dz_first = sb.tile([P, HALF * PACK], BF16, name="dz_first", tag="dz_bf", align_bytes=64)
+        w_late = sb.tile([P, HALF * PACK], BF16, name="w_late", align_bytes=64)
+        wcut = 96
         nc.scalar.activation(out=w_dst[:, 0:wcut], in_=w_src[:, 0:wcut, :, 0:2], func=ACT.Copy)
-        weave_dz(nc.scalar.copy, dz_bf[0], 0, 0, P)
+        weave_dz(nc.scalar.copy, dz_first, 0, 0, P)
+        weave_dz(nc.vector.tensor_copy, dz_first, 0, P, HALF)
         nc.scalar.activation(out=w_dst[:, wcut:P], in_=w_src[:, wcut:P, :, 0:2], func=ACT.Copy)
-        weave_dz(nc.scalar.copy, dz_bf[1], P, P, HALF)
-        quantise(nc, grad_codes, grad_scales, dz_bf[0], E5M2, 0, P, shift=N)
-        for t in range(2):
-            quantise(nc, w_codes, w_scales, w_bf, E4M3, t * P, (t + 1) * P)
-        quantise(nc, grad_codes, grad_scales, dz_bf[1], E5M2, 0, P, shift=N + P)
-        dz_rest = sb.tile([P, HALF * PACK], BF16, name="dz_rest", tag="w_bf", align_bytes=64)
-        for c0 in (HALF, HALF + P):
-            weave_dz(nc.vector.tensor_copy, dz_rest, HALF, c0, c0 + P)
-        for c0 in (0, P):
-            quantise(nc, grad_codes, grad_scales, dz_rest, E5M2, c0, c0 + P, shift=N + HALF)
-
-        w_late = sb.tile([P, HALF * PACK], BF16, name="w_late", tag="dz_bf0", align_bytes=64)
         nc.scalar.activation(
             out=w_late[:].rearrange("p (t m j) -> p m j t", t=2, j=PACK), in_=w_src[:, :, :, 2:4], func=ACT.Copy
         )
+        quantise(nc, grad_codes, grad_scales, dz_first, E5M2, 0, HALF, shift=N)
+        quantise(nc, w_codes, w_scales, w_bf, E4M3, 0, HALF)
+        dz_rest = sb.tile([P, HALF * PACK], BF16, name="dz_rest", tag="dz_bf", align_bytes=64)
+        dcut = HALF + 160
+        weave_dz(nc.vector.tensor_copy, dz_rest, HALF, HALF, dcut)
+        weave_dz(nc.scalar.copy, dz_rest, HALF, dcut, N)
         quantise(nc, w_codes, w_scales, w_late, E4M3, 0, HALF, shift=HALF)
+        quantise(nc, grad_codes, grad_scales, dz_rest, E5M2, 0, HALF, shift=N + HALF)
 
         y = [sb.tile([P, PACK, HALF], F32, name="y%d" % a) for a in range(2)]
         y_rows = out_0.rearrange("(p t) c -> p t c", t=PACK)
@@ -234,26 +231,30 @@ def tile_attend_ghsort_tnh_pl_kernel(tc, wo, dyT, W, h, offs, out_0, out_1, out_
         def weave_y(copy, a, c0, c1):
             copy(out=weave(y_bf, a * HALF + c0, a * HALF + c1), in_=runs(y[a], c0, c1))
 
-        planes("early0", 0, 0, 2, nc.scalar.copy)
-        store(0, 0, 2)
-        planes("early1", 1, 0, 2, nc.vector.tensor_copy)
-        store(1, 0, 2)
-        planes("bank0", 0, 2, 3, nc.scalar.copy)
-        planes("bank1", 0, 3, 4, nc.scalar.copy)
-        store(0, 2, 4)
-        planes("bank2", 1, 2, 3, nc.scalar.copy)
-        planes("bank3", 1, 3, 4, nc.scalar.copy)
-        store(1, 2, 4)
-        ycut = 160
-        weave_y(nc.vector.tensor_copy, 0, 0, HALF)
-        weave_y(nc.vector.tensor_copy, 1, 0, ycut)
-        weave_y(nc.scalar.copy, 1, ycut, HALF)
         words = out_1.rearrange("g p c l -> (g p) (c l)").bitcast(I32)
-        for a in range(2):
+
+        def hand_on(a):
             quantise(nc, y_codes, y_scales, y_bf, E4M3, a * HALF, (a + 1) * HALF)
             nc.sync.dma_start(
                 out=words[:, a * HALF : (a + 1) * HALF], in_=y_codes[:, a * HALF : (a + 1) * HALF].bitcast(I32)
             )
+
+        planes("early0", 0, 0, 2, nc.scalar.copy)
+        store(0, 0, 2)
+        planes("bank0", 0, 2, 3, nc.vector.tensor_copy)
+        planes("bank1", 0, 3, 4, nc.scalar.copy)
+        store(0, 2, 4)
+        weave_y(nc.vector.tensor_copy, 0, 0, HALF)
+        planes("early1", 1, 0, 2, nc.scalar.copy)
+        store(1, 0, 2)
+        planes("bank2", 1, 2, 3, nc.vector.tensor_copy)
+        planes("bank3", 1, 3, 4, nc.scalar.copy)
+        store(1, 2, 4)
+        hand_on(0)
+        ycut = 160
+        weave_y(nc.vector.tensor_copy, 1, 0, ycut)
+        weave_y(nc.scalar.copy, 1, ycut, HALF)
+        hand_on(1)
         rows = out_2.rearrange("g q c -> (g q) c").bitcast(I32)
         for q in range(4):
             engine = nc.scalar if q % 2 == 0 else nc.sync

@@ -20,20 +20,27 @@ HALF = N // 2
 FLOPS = 2 * 2 * N * N * N
 
 
-def quantise(nc, codes, scales, grouped, fmt, c0, c1, shift=0):
-    nc.vector.quantize_mx(
-        out=codes[:, shift + c0 : shift + c1].bitcast(fmt),
-        scales=scales[:, shift + c0 : shift + c1],
-        in_=grouped[:, c0 * PACK : c1 * PACK],
+def quantise(nc, codes, scales, grouped, fmt):
+    nc.vector.quantize_mx(out=codes.bitcast(fmt), scales=scales, in_=grouped)
+
+
+def weave(copy, tile, planes, c0, c1):
+    copy(
+        out=tile[:, c0 * PACK : c1 * PACK].rearrange("p (c i j) -> p c j i", i=4, j=PACK),
+        in_=planes[:, :, c0:c1].rearrange("p j (c i) -> p c j i", i=4),
     )
 
 
-def weave(tile, c0, c1):
-    return tile[:, c0 * PACK : c1 * PACK].rearrange("p (c i j) -> p c j i", i=4, j=PACK)
-
-
-def runs(planes, c0, c1):
-    return planes[:, :, c0:c1].rearrange("p j (c i) -> p c j i", i=4)
+def product(nc, out, w_codes, w_scales, g_codes, g_scales):
+    nc.tensor.matmul_mx(
+        out=out,
+        lhsT=w_codes.bitcast(E4M3),
+        lhsT_scale=w_scales,
+        rhs=g_codes.bitcast(E5M2),
+        rhs_scale=g_scales,
+        start=True,
+        stop=True,
+    )
 
 
 def tile_attend_ghsort_tnh_pl_kernel(tc, wo, dyT, W, h, offs, out_0, out_1, out_2):
@@ -42,219 +49,195 @@ def tile_attend_ghsort_tnh_pl_kernel(tc, wo, dyT, W, h, offs, out_0, out_1, out_
         sb = ctx.enter_context(tc.tile_pool(name="sb", bufs=1))
         ps = ctx.enter_context(tc.psum_pool(name="ps", bufs=1))
 
+        def tile(name, shape, dtype, tag=None):
+            return sb.tile(shape, dtype, name=name, tag=tag or name, align_bytes=64)
+
+        def bank(k, shape):
+            return ps.tile(shape, F32, name="bank", tag="bank%d" % k)
+
+        def scalar_cast(out, in_):
+            nc.scalar.activation(out=out, in_=in_, func=ACT.Copy)
+
         offsets = sb.tile([P, N // 16], U16, name="offsets")
-        wo_raw = sb.tile([P, PACK, N], F32, name="wo_raw")
-        dy_raw = sb.tile([P, PACK, N], F32, name="dy_raw")
+        dy_raw = tile("dy_raw", [P, PACK, N], F32)
+        wo_raw = tile("wo_raw", [P, PACK, N], F32)
         h_cuts = (0, 640, 1280, PACK * N)
-        h_part = [sb.tile([P, h_cuts[a + 1] - h_cuts[a]], F32, name="h_part%d" % a) for a in range(3)]
-        w_raw = sb.tile([P, PACK, N], F32, name="w_raw")
+        h_part = [tile("h_part%d" % a, [P, h_cuts[a + 1] - h_cuts[a]], F32) for a in range(3)]
+        w_raw = tile("w_raw", [P, PACK, N], F32)
 
         h_rows = h.rearrange("(p j) c -> p (j c)", j=PACK)
         nc.sync.dma_start(out=dy_raw[:], in_=dyT.rearrange("(p j) c -> p j c", j=PACK))
         nc.sync.dma_start(out=wo_raw[:], in_=wo.rearrange("(p j) c -> p j c", j=PACK))
-        for a in range(2):
+        for a in range(3):
             nc.sync.dma_start(out=h_part[a][:], in_=h_rows[:, h_cuts[a] : h_cuts[a + 1]])
-        nc.sync.dma_start(offsets[:], offs)
-        nc.sync.dma_start(out=h_part[2][:], in_=h_rows[:, h_cuts[2] : h_cuts[3]])
+            if a == 1:
+                nc.sync.dma_start(offsets[:], offs)
         nc.sync.dma_start(out=w_raw[:], in_=W.rearrange("(p j) c -> p j c", j=PACK))
 
-        def operand(name):
-            grouped = sb.tile([P, N * PACK], BF16, name=name + "_bf", tag=name + "_bf", align_bytes=64)
-            codes = sb.tile([P, N], U32, name=name + "_codes", tag=name + "_codes", align_bytes=64)
-            scales = sb.tile([P, N], U8, name=name + "_scales", tag=name + "_scales", align_bytes=64)
-            return grouped, codes, scales
-
-        w_codes = sb.tile([P, N], U32, name="w_codes", align_bytes=64)
-        w_scales = sb.tile([P, N], U8, name="w_scales", align_bytes=64)
-        w_bf = sb.tile([P, 2 * P * PACK], BF16, name="w_bf", tag="w_bf", align_bytes=64)
-        dy_bf = sb.tile([P, N * PACK], BF16, name="dy_bf", align_bytes=64)
-        grad_codes = sb.tile([P, 2 * N], U32, name="grad_codes", align_bytes=64)
-        grad_scales = sb.tile([P, 2 * N], U8, name="grad_scales", align_bytes=64)
-        y_bf, y_codes, y_scales = operand("y")
-        wo_bf = sb.tile([P, N * PACK], BF16, name="wo_bf", align_bytes=64)
-        wo_scales = sb.tile([P, N], U8, name="wo_scales", align_bytes=64)
-        wo_codes = [
-            sb.tile([P, width], U32, name="wo_codes", tag="wo_codes%d" % a, align_bytes=64)
-            for a, width in enumerate((P, P, HALF))
-        ]
-        wo_plane = [wo_codes[0][:], wo_codes[1][:], wo_codes[2][:, 0:P], wo_codes[2][:, P:HALF]]
-
+        dy_bf = tile("dy_bf", [P, N * PACK], BF16)
+        dy_codes = tile("dy_codes", [P, N], U32)
+        dy_scales = tile("dy_scales", [P, N], U8)
         cut = 320
-        nc.vector.tensor_copy(out=weave(dy_bf, 0, cut), in_=runs(dy_raw, 0, cut))
-        nc.scalar.activation(out=weave(dy_bf, cut, N), in_=runs(dy_raw, cut, N), func=ACT.Copy)
-        quantise(nc, grad_codes, grad_scales, dy_bf, E5M2, 0, N)
+        weave(nc.vector.tensor_copy, dy_bf, dy_raw, 0, cut)
+        weave(scalar_cast, dy_bf, dy_raw, cut, N)
+        quantise(nc, dy_codes[:], dy_scales[:], dy_bf[:], E5M2)
 
-        def quantise_wo(a, c0, c1):
-            nc.vector.quantize_mx(
-                out=wo_codes[a][:].bitcast(E4M3), scales=wo_scales[:, c0:c1], in_=wo_bf[:, c0 * PACK : c1 * PACK]
-            )
-
+        wo_bf = tile("wo_bf", [P, N * PACK], BF16)
+        wo_cuts = (0, P, HALF, N)
+        wo_codes = [tile("wo_codes%d" % a, [P, wo_cuts[a + 1] - wo_cuts[a]], U32) for a in range(3)]
+        wo_plane = [wo_codes[0][:], wo_codes[1][:], wo_codes[2][:, 0:P], wo_codes[2][:, P:HALF]]
+        wo_scales = tile("wo_scales", [P, N], U8)
         wo_dst = wo_bf[:].rearrange("p (t m j) -> p m j t", t=PACK, j=PACK)
         wo_src = wo_raw[:].rearrange("p j (m t) -> p m j t", t=PACK)
+
+        def quantise_wo(a):
+            c0, c1 = wo_cuts[a], wo_cuts[a + 1]
+            quantise(nc, wo_codes[a][:], wo_scales[:, c0:c1], wo_bf[:, c0 * PACK : c1 * PACK], E4M3)
+
         mcut = 76
         nc.vector.tensor_copy(out=wo_dst[:, 0:mcut, :, 0:2], in_=wo_src[:, 0:mcut, :, 0:2])
-        nc.scalar.activation(out=wo_dst[:, mcut:P, :, 0:2], in_=wo_src[:, mcut:P, :, 0:2], func=ACT.Copy)
-        quantise_wo(0, 0, P)
-        quantise_wo(1, P, HALF)
+        scalar_cast(wo_dst[:, mcut:P, :, 0:2], wo_src[:, mcut:P, :, 0:2])
+        quantise_wo(0)
+        quantise_wo(1)
         nc.vector.tensor_copy(out=wo_dst[:, :, :, 2:4], in_=wo_src[:, :, :, 2:4])
 
-        slopes = sb.tile([P, PACK * N], F32, name="slopes", align_bytes=64)
-        slope = [slopes[:, t * N : (t + 1) * N] for t in range(PACK)]
+        slopes = tile("slopes", [P, PACK * N], F32)
+        squares = {}
 
-        def square(source, width, tag):
-            sq = sb.tile([P, width], F32, name="sq", tag=tag, align_bytes=64)
-            nc.scalar.activation(out=sq[:], in_=source, func=ACT.Square)
-            return sq
+        def square(a):
+            tag = ("squares0", "squares1", "wo_codes1")[a]
+            squares[a] = tile("squares%d" % a, [P, h_cuts[a + 1] - h_cuts[a]], F32, tag=tag)
+            nc.scalar.activation(out=squares[a][:], in_=h_part[a][:], func=ACT.Square)
 
-        def affine(out, squares):
-            nc.vector.tensor_scalar(out=out, in0=squares, scalar1=-1.0, scalar2=1.0, op0=ALU.mult, op1=ALU.add)
-
-        sq_head = [square(h_part[a][:], h_cuts[1], "sq%d" % a) for a in range(2)]
-        affine(slopes[:, 0 : h_cuts[1]], sq_head[0][:])
-        quantise_wo(2, HALF, N)
-        affine(slopes[:, h_cuts[1] : h_cuts[2]], sq_head[1][:])
-
-        def product(tag, codes, scales, c0):
-            bank = ps.tile([P, N], F32, name="bank", tag=tag)
-            nc.tensor.matmul_mx(
-                out=bank[:],
-                lhsT=codes.bitcast(E4M3),
-                lhsT_scale=scales,
-                rhs=grad_codes[:, c0 : c0 + N].bitcast(E5M2),
-                rhs_scale=grad_scales[:, c0 : c0 + N],
-                start=True,
-                stop=True,
+        def affine_vector(a):
+            nc.vector.tensor_scalar(
+                out=slopes[:, h_cuts[a] : h_cuts[a + 1]], in0=squares[a][:], scalar1=-1.0, scalar2=1.0, op0=ALU.mult, op1=ALU.add
             )
-            return bank
 
-        banks_u = [product("bank%d" % t, wo_plane[t], wo_scales[:, t * P : (t + 1) * P], 0) for t in range(PACK)]
-
-        u = [sb.tile([P, 2 * N], F32, name="u%d" % t) for t in range(2)]
-        for t in range(2):
-            nc.vector.memset(u[t][:, N : 2 * N], 0.0)
-        u.append(sb.tile([P, N], F32, name="u2"))
-        u.append(sb.tile([P, N], F32, name="u3", tag="u3", align_bytes=64))
-        dz = sb.tile([P, 7 * N], F32, name="dz")
-
-        def dz_at(t, c0, c1):
-            first = t * N + (3 * HALF if t >= 2 and c0 >= HALF else 0)
-            return dz[:, first + c0 : first + c1]
-
-
-        def fetch(t):
-            nc.vector.tensor_tensor(out=dz_at(t, 0, N), in0=u[t][:].indirect(offsets[:]), in1=slope[t], op=ALU.mult)
-
-        for t in range(2):
-            nc.scalar.copy(out=u[t][:, 0:N], in_=banks_u[t][:])
-            fetch(t)
-        sq_late = square(h_part[2][:], 3 * HALF, "wo_codes1")
-
-        def affine_scalar(k):
+        def affine_scalar(a, c0, c1):
             nc.scalar.activation(
-                out=slopes[:, h_cuts[2] + k * HALF : h_cuts[2] + (k + 1) * HALF],
-                in_=sq_late[:, k * HALF : (k + 1) * HALF],
+                out=slopes[:, h_cuts[a] + c0 : h_cuts[a] + c1],
+                in_=squares[a][:, c0:c1],
                 func=ACT.Identity,
                 scale=-1.0,
                 bias=1.0,
             )
 
-        nc.scalar.copy(out=u[2][:], in_=banks_u[2][:])
-        affine_scalar(1)
-        nc.scalar.copy(out=u[3][:], in_=banks_u[3][:])
-        affine_scalar(0)
-        affine_scalar(2)
+        dz_flat = tile("dz", [P, 7 * N], F32)
 
-        def fetch_part(t, c0, c1):
+        def dz_half(a):
+            span = 2 * N + 3 * HALF * a
+            pairs = dz_flat[:, 0 : 2 * span].rearrange("p (a s) -> p a s", a=2)
+            return pairs[:, :, 0 : 2 * N].rearrange("p a (b c) -> p a b c", b=2)[:, :, :, a * HALF : (a + 1) * HALF]
+
+        def weave_dz(copy, dst, a, c0, c1):
+            copy(
+                out=dst.rearrange("p (c i a b) -> p c a b i", i=4, a=2, b=2),
+                in_=dz_half(a)[:, :, :, c0:c1].rearrange("p a b (c i) -> p c a b i", i=4),
+            )
+
+        def fetch(t, c0, c1):
+            first = t * N + (3 * HALF if t >= 2 and c0 >= HALF else 0)
             nc.vector.tensor_tensor(
-                out=dz_at(t, c0, c1),
+                out=dz_flat[:, first + c0 : first + c1],
                 in0=u[t][:].indirect(offsets[:, c0 // 16 : c1 // 16]),
-                in1=slope[t][:, c0:c1],
+                in1=slopes[:, t * N + c0 : t * N + c1],
                 op=ALU.mult,
             )
 
-        def weave_dz(copy, tile, first, c0, c1):
-            span = 2 * N + (3 * HALF if c0 >= HALF else 0)
-            pairs = dz[:, 0 : 2 * span].rearrange("p (a s) -> p a s", a=2)
-            lanes = pairs[:, :, 0 : 2 * N].rearrange("p a (b c) -> p a b c", b=2)[:, :, :, c0:c1]
-            copy(
-                out=tile[:, (c0 - first) * PACK : (c1 - first) * PACK].rearrange("p (c i a b) -> p c a b i", i=4, a=2, b=2),
-                in_=lanes.rearrange("p a b (c i) -> p c a b i", i=4),
-            )
+        for a in range(2):
+            square(a)
+        affine_vector(0)
+        quantise_wo(2)
+        affine_vector(1)
 
-        def product_w(out, t, c0, c1):
-            nc.tensor.matmul_mx(
-                out=out,
-                lhsT=w_codes[:, t * P : (t + 1) * P].bitcast(E4M3),
-                lhsT_scale=w_scales[:, t * P : (t + 1) * P],
-                rhs=grad_codes[:, N + c0 : N + c1].bitcast(E5M2),
-                rhs_scale=grad_scales[:, N + c0 : N + c1],
-                start=True,
-                stop=True,
-            )
+        banks_u = [bank(t, [P, N]) for t in range(PACK)]
+        for t in range(PACK):
+            product(nc, banks_u[t][:], wo_plane[t], wo_scales[:, t * P : (t + 1) * P], dy_codes[:], dy_scales[:])
 
+        u = [tile("u%d" % t, [P, 2 * N if t < 2 else N], F32) for t in range(PACK)]
+        for t in range(2):
+            nc.vector.memset(u[t][:, N : 2 * N], 0.0)
+        for t in range(2):
+            nc.scalar.copy(out=u[t][:, 0:N], in_=banks_u[t][:])
+            fetch(t, 0, N)
+        square(2)
+        for t, pieces in ((2, (1,)), (3, (0, 2))):
+            nc.scalar.copy(out=u[t][:], in_=banks_u[t][:])
+            for k in pieces:
+                affine_scalar(2, k * HALF, (k + 1) * HALF)
         for a in range(2):
             for t in range(2, PACK):
-                fetch_part(t, a * HALF, (a + 1) * HALF)
-        w_dst = w_bf[:].rearrange("p (t m j) -> p m j t", t=2, j=PACK)
+                fetch(t, a * HALF, (a + 1) * HALF)
+
+        w_codes = tile("w_codes", [P, N], U32)
+        w_scales = tile("w_scales", [P, N], U8)
+        w_bf = [tile("w_bf%d" % a, [P, HALF * PACK], BF16) for a in range(2)]
+
         w_src = w_raw[:].rearrange("p j (m t) -> p m j t", t=PACK)
-        dz_first = sb.tile([P, HALF * PACK], BF16, name="dz_first", tag="dz_bf", align_bytes=64)
-        w_late = sb.tile([P, HALF * PACK], BF16, name="w_late", align_bytes=64)
-        wcut = 96
-        nc.scalar.activation(out=w_dst[:, 0:wcut], in_=w_src[:, 0:wcut, :, 0:2], func=ACT.Copy)
-        weave_dz(nc.scalar.copy, dz_first, 0, 0, P)
-        weave_dz(nc.vector.tensor_copy, dz_first, 0, P, HALF)
-        nc.scalar.activation(out=w_dst[:, wcut:P], in_=w_src[:, wcut:P, :, 0:2], func=ACT.Copy)
-        nc.scalar.activation(
-            out=w_late[:].rearrange("p (t m j) -> p m j t", t=2, j=PACK), in_=w_src[:, :, :, 2:4], func=ACT.Copy
-        )
-        quantise(nc, grad_codes, grad_scales, dz_first, E5M2, 0, HALF, shift=N)
-        quantise(nc, w_codes, w_scales, w_bf, E4M3, 0, HALF)
-        dz_rest = sb.tile([P, HALF * PACK], BF16, name="dz_rest", tag="dz_bf", align_bytes=64)
-        dcut = HALF + 160
-        weave_dz(nc.vector.tensor_copy, dz_rest, HALF, HALF, dcut)
-        weave_dz(nc.scalar.copy, dz_rest, HALF, dcut, N)
-        quantise(nc, w_codes, w_scales, w_late, E4M3, 0, HALF, shift=HALF)
-        quantise(nc, grad_codes, grad_scales, dz_rest, E5M2, 0, HALF, shift=N + HALF)
 
-        y = [sb.tile([P, PACK, HALF], F32, name="y%d" % a) for a in range(2)]
+        def cast_w(a):
+            scalar_cast(w_bf[a][:].rearrange("p (t m j) -> p m j t", t=2, j=PACK), w_src[:, :, :, 2 * a : 2 * a + 2])
+
+        dz_codes = tile("dz_codes", [P, N], U32)
+        dz_scales = tile("dz_scales", [P, N], U8)
+
+        def quantise_dz(grouped, c0, c1):
+            quantise(nc, dz_codes[:, c0:c1], dz_scales[:, c0:c1], grouped, E5M2)
+
+        cast_w(0)
+        dz_first = tile("dz_first", [P, HALF * PACK], BF16)
+        dcut = 48
+        weave_dz(nc.scalar.copy, dz_first[:, 0 : dcut * PACK], 0, 0, dcut)
+        weave_dz(nc.vector.tensor_copy, dz_first[:, dcut * PACK : HALF * PACK], 0, dcut, HALF)
+        cast_w(1)
+        quantise_dz(dz_first[:], 0, HALF)
+        quantise(nc, w_codes[:, 0:HALF], w_scales[:, 0:HALF], w_bf[0][:], E4M3)
+        dz_rest = tile("dz_rest", [P, HALF * PACK], BF16, tag="w_raw")
+        dz_third, dz_last = dz_rest[:, 0:N], dz_rest[:, N : 2 * N]
+        weave_dz(nc.scalar.copy, dz_third, 1, 0, P)
+        quantise(nc, w_codes[:, HALF:N], w_scales[:, HALF:N], w_bf[1][:], E4M3)
+        weave_dz(nc.vector.tensor_copy, dz_last, 1, P, HALF)
+        quantise_dz(dz_third, HALF, HALF + P)
+        quantise_dz(dz_last, HALF + P, N)
+
         y_rows = out_0.rearrange("(p t) c -> p t c", t=PACK)
-
-        def planes(tag, a, t0, t1, copy):
-            bank = ps.tile([P, t1 - t0, HALF], F32, name="bank", tag=tag)
-            for t in range(t0, t1):
-                product_w(bank[:, t - t0, :], t, a * HALF, (a + 1) * HALF)
-            copy(out=y[a][:, t0:t1, :], in_=bank[:])
-
-        def store(a, t0, t1):
-            nc.sync.dma_start(out=y_rows[:, t0:t1, a * HALF : (a + 1) * HALF], in_=y[a][:, t0:t1, :])
-
-        def weave_y(copy, a, c0, c1):
-            copy(out=weave(y_bf, a * HALF + c0, a * HALF + c1), in_=runs(y[a], c0, c1))
-
         words = out_1.rearrange("g p c l -> (g p) (c l)").bitcast(I32)
+        y_codes = tile("y_codes", [P, N], U32)
+        y_scales = tile("y_scales", [P, N], U8)
+        y = [tile("y%d" % a, [P, PACK, HALF], F32, tag=("w_bf1", "y1")[a]) for a in range(2)]
+        for a, (first, cuts) in enumerate(((4, (0, 1, 2, 3, 4)), (0, (0, 1, 2, 3, 4)))):
+            cols = slice(a * HALF, (a + 1) * HALF)
+            for k, (t0, t1) in enumerate(zip(cuts, cuts[1:])):
+                copy = nc.vector.tensor_copy if (a, t0) == (1, 0) else nc.scalar.copy
+                planes = bank(first + k, [P, t1 - t0, HALF])
+                for t in range(t0, t1):
+                    m = slice(t * P, (t + 1) * P)
+                    product(nc, planes[:, t - t0, :], w_codes[:, m], w_scales[:, m], dz_codes[:, cols], dz_scales[:, cols])
+                copy(out=y[a][:, t0:t1, :], in_=planes[:])
+                if (a, t0) == (0, 0) or t1 % 2 == 0:
+                    t0 = t0 if (a, t0) in ((0, 0), (0, 1)) else t1 - 2
+                    nc.sync.dma_start(out=y_rows[:, t0:t1, cols], in_=y[a][:, t0:t1, :])
+        y_bf = [tile("y_bf%d" % a, [P, PACK * HALF], BF16) for a in range(2)]
 
-        def hand_on(a):
-            quantise(nc, y_codes, y_scales, y_bf, E4M3, a * HALF, (a + 1) * HALF)
-            nc.sync.dma_start(
-                out=words[:, a * HALF : (a + 1) * HALF], in_=y_codes[:, a * HALF : (a + 1) * HALF].bitcast(I32)
-            )
+        def quantise_y(a, c0, c1):
+            cols = slice(a * HALF + c0, a * HALF + c1)
+            quantise(nc, y_codes[:, cols], y_scales[:, cols], y_bf[a][:, c0 * PACK : c1 * PACK], E4M3)
 
-        planes("early0", 0, 0, 2, nc.scalar.copy)
-        store(0, 0, 2)
-        planes("bank0", 0, 2, 3, nc.vector.tensor_copy)
-        planes("bank1", 0, 3, 4, nc.scalar.copy)
-        store(0, 2, 4)
-        weave_y(nc.vector.tensor_copy, 0, 0, HALF)
-        planes("early1", 1, 0, 2, nc.scalar.copy)
-        store(1, 0, 2)
-        planes("bank2", 1, 2, 3, nc.vector.tensor_copy)
-        planes("bank3", 1, 3, 4, nc.scalar.copy)
-        store(1, 2, 4)
-        hand_on(0)
-        ycut = 160
-        weave_y(nc.vector.tensor_copy, 1, 0, ycut)
-        weave_y(nc.scalar.copy, 1, ycut, HALF)
-        hand_on(1)
+        def store_words(a):
+            cols = slice(a * HALF, (a + 1) * HALF)
+            nc.sync.dma_start(out=words[:, cols], in_=y_codes[:, cols].bitcast(I32))
+
+        for c0 in (0, P):
+            weave(nc.vector.tensor_copy, y_bf[0], y[0], c0, c0 + P)
+        quantise_y(0, 0, P)
+        weave(nc.scalar.copy, y_bf[1], y[1], 0, P)
+        weave(nc.vector.tensor_copy, y_bf[1], y[1], P, HALF)
+        quantise_y(0, P, HALF)
+        store_words(0)
+        for c0 in (0, P):
+            quantise_y(1, c0, c0 + P)
+        store_words(1)
         rows = out_2.rearrange("g q c -> (g q) c").bitcast(I32)
         for q in range(4):
             engine = nc.scalar if q % 2 == 0 else nc.sync

@@ -47,6 +47,7 @@ def tile_attend_ghsort_tnh_pl_kernel(tc, wo, dyT, W, h, offs, out_0, out_1, out_
     nc = tc.nc
     with ExitStack() as ctx:
         sb = ctx.enter_context(tc.tile_pool(name="sb", bufs=1))
+        shared = ctx.enter_context(tc.tile_pool(name="shared", bufs=1))
         ps = ctx.enter_context(tc.psum_pool(name="ps", bufs=1))
 
         def tile(name, shape, dtype, tag=None):
@@ -63,7 +64,7 @@ def tile_attend_ghsort_tnh_pl_kernel(tc, wo, dyT, W, h, offs, out_0, out_1, out_
         wo_raw = tile("wo_raw", [P, PACK, N], F32)
         h_cuts = (0, 640, 1280, PACK * N)
         h_part = [tile("h_part%d" % a, [P, h_cuts[a + 1] - h_cuts[a]], F32) for a in range(3)]
-        w_raw = tile("w_raw", [P, PACK, N], F32)
+        w_raw = shared.tile([P, PACK, N], F32, name="w_raw", offset=0, align_bytes=64)
 
         h_rows = h.rearrange("(p j) c -> p (j c)", j=PACK)
         nc.sync.dma_start(out=dy_raw[:], in_=dyT.rearrange("(p j) c -> p j c", j=PACK))
@@ -162,13 +163,30 @@ def tile_attend_ghsort_tnh_pl_kernel(tc, wo, dyT, W, h, offs, out_0, out_1, out_
             nc.scalar.copy(out=u[t][:, 0:N], in_=banks_u[t][:])
             fetch(t, 0, N)
         square(2)
-        for t, pieces in ((2, (1,)), (3, (0, 2))):
+        for t, pieces in ((2, (1,)), (3, ())):
             nc.scalar.copy(out=u[t][:], in_=banks_u[t][:])
             for k in pieces:
                 affine_scalar(2, k * HALF, (k + 1) * HALF)
-        for a in range(2):
-            for t in range(2, PACK):
-                fetch(t, a * HALF, (a + 1) * HALF)
+        negated = {}
+        for t in range(2, PACK):
+            negated[t] = tile("negated%d" % t, [P, HALF], F32)
+            nc.scalar.activation(
+                out=negated[t][:], in_=u[t][:].indirect(offsets[:, HALF // 16 : N // 16]), func=ACT.Copy, scale=-1.0
+            )
+        for t in range(2, PACK):
+            fetch(t, 0, HALF)
+
+        def finish(t):
+            first = t * N + 4 * HALF
+            k = 2 * (t - 2)
+            nc.vector.scalar_tensor_tensor(
+                out=dz_flat[:, first : first + HALF],
+                in0=squares[2][:, k * HALF : (k + 1) * HALF],
+                scalar=1.0,
+                in1=negated[t][:],
+                op0=ALU.subtract,
+                op1=ALU.mult,
+            )
 
         w_codes = tile("w_codes", [P, N], U32)
         w_scales = tile("w_scales", [P, N], U8)
@@ -176,8 +194,9 @@ def tile_attend_ghsort_tnh_pl_kernel(tc, wo, dyT, W, h, offs, out_0, out_1, out_
 
         w_src = w_raw[:].rearrange("p j (m t) -> p m j t", t=PACK)
 
-        def cast_w(a):
-            scalar_cast(w_bf[a][:].rearrange("p (t m j) -> p m j t", t=2, j=PACK), w_src[:, :, :, 2 * a : 2 * a + 2])
+        def cast_w(cast, a, m0, m1):
+            dst = w_bf[a][:].rearrange("p (t m j) -> p m j t", t=2, j=PACK)
+            cast(out=dst[:, m0:m1], in_=w_src[:, m0:m1, :, 2 * a : 2 * a + 2])
 
         dz_codes = tile("dz_codes", [P, N], U32)
         dz_scales = tile("dz_scales", [P, N], U8)
@@ -185,18 +204,22 @@ def tile_attend_ghsort_tnh_pl_kernel(tc, wo, dyT, W, h, offs, out_0, out_1, out_
         def quantise_dz(grouped, c0, c1):
             quantise(nc, dz_codes[:, c0:c1], dz_scales[:, c0:c1], grouped, E5M2)
 
-        cast_w(0)
+        cast_w(scalar_cast, 0, 0, P)
         dz_first = tile("dz_first", [P, HALF * PACK], BF16)
-        dcut = 48
-        weave_dz(nc.scalar.copy, dz_first[:, 0 : dcut * PACK], 0, 0, dcut)
-        weave_dz(nc.vector.tensor_copy, dz_first[:, dcut * PACK : HALF * PACK], 0, dcut, HALF)
-        cast_w(1)
+        finish(2)
+        weave_dz(nc.vector.tensor_copy, dz_first[:], 0, 0, HALF)
+        finish(3)
+        wcut = 56
+        cast_w(scalar_cast, 1, wcut, P)
+        cast_w(nc.vector.tensor_copy, 1, 0, wcut)
         quantise_dz(dz_first[:], 0, HALF)
         quantise(nc, w_codes[:, 0:HALF], w_scales[:, 0:HALF], w_bf[0][:], E4M3)
-        dz_rest = tile("dz_rest", [P, HALF * PACK], BF16, tag="w_raw")
-        dz_third, dz_last = dz_rest[:, 0:N], dz_rest[:, N : 2 * N]
+        third = shared.tile([P, N], BF16, name="dz_third", offset=0, align_bytes=64)
+        dz_third = third[:]
         weave_dz(nc.scalar.copy, dz_third, 1, 0, P)
         quantise(nc, w_codes[:, HALF:N], w_scales[:, HALF:N], w_bf[1][:], E4M3)
+        last = shared.tile([P, N], BF16, name="dz_last", offset=1024, align_bytes=64)
+        dz_last = last[:]
         weave_dz(nc.vector.tensor_copy, dz_last, 1, P, HALF)
         quantise_dz(dz_third, HALF, HALF + P)
         quantise_dz(dz_last, HALF + P, N)
@@ -205,11 +228,14 @@ def tile_attend_ghsort_tnh_pl_kernel(tc, wo, dyT, W, h, offs, out_0, out_1, out_
         words = out_1.rearrange("g p c l -> (g p) (c l)").bitcast(I32)
         y_codes = tile("y_codes", [P, N], U32)
         y_scales = tile("y_scales", [P, N], U8)
-        y = [tile("y%d" % a, [P, PACK, HALF], F32, tag=("w_bf1", "y1")[a]) for a in range(2)]
+        y = [
+            shared.tile([P, PACK, HALF], F32, name="y0", offset=4096, align_bytes=64),
+            tile("y1", [P, PACK, HALF], F32),
+        ]
         for a, (first, cuts) in enumerate(((4, (0, 1, 2, 3, 4)), (0, (0, 1, 2, 3, 4)))):
             cols = slice(a * HALF, (a + 1) * HALF)
             for k, (t0, t1) in enumerate(zip(cuts, cuts[1:])):
-                copy = nc.vector.tensor_copy if (a, t0) == (1, 0) else nc.scalar.copy
+                copy = nc.vector.tensor_copy if (a, t0) in ((0, 3), (1, 2)) else nc.scalar.copy
                 planes = bank(first + k, [P, t1 - t0, HALF])
                 for t in range(t0, t1):
                     m = slice(t * P, (t + 1) * P)

@@ -241,8 +241,8 @@ def tile_attend_ghsort_tnh_pl_kernel(tc, wo, dyT, W, h, offs, out_0, out_1, out_
                     m = slice(t * P, (t + 1) * P)
                     product(nc, planes[:, t - t0, :], w_codes[:, m], w_scales[:, m], dz_codes[:, cols], dz_scales[:, cols])
                 copy(out=y[a][:, t0:t1, :], in_=planes[:])
-                if (a, t0) == (0, 0) or t1 % 2 == 0:
-                    t0 = t0 if (a, t0) in ((0, 0), (0, 1)) else t1 - 2
+                if a == 0 or t1 % 2 == 0:
+                    t0 = t1 - 1 - a
                     nc.sync.dma_start(out=y_rows[:, t0:t1, cols], in_=y[a][:, t0:t1, :])
         y_bf = [tile("y_bf%d" % a, [P, PACK * HALF], BF16) for a in range(2)]
 
@@ -250,20 +250,15 @@ def tile_attend_ghsort_tnh_pl_kernel(tc, wo, dyT, W, h, offs, out_0, out_1, out_
             cols = slice(a * HALF + c0, a * HALF + c1)
             quantise(nc, y_codes[:, cols], y_scales[:, cols], y_bf[a][:, c0 * PACK : c1 * PACK], E4M3)
 
-        def store_words(a):
-            cols = slice(a * HALF, (a + 1) * HALF)
-            nc.sync.dma_start(out=words[:, cols], in_=y_codes[:, cols].bitcast(I32))
-
         for c0 in (0, P):
             weave(nc.vector.tensor_copy, y_bf[0], y[0], c0, c0 + P)
         quantise_y(0, 0, P)
         weave(nc.scalar.copy, y_bf[1], y[1], 0, P)
         weave(nc.vector.tensor_copy, y_bf[1], y[1], P, HALF)
         quantise_y(0, P, HALF)
-        store_words(0)
         for c0 in (0, P):
             quantise_y(1, c0, c0 + P)
-        store_words(1)
+        nc.sync.dma_start(out=words, in_=y_codes[:].bitcast(I32))
         rows = out_2.rearrange("g q c -> (g q) c").bitcast(I32)
         for q in range(4):
             engine = nc.scalar if q % 2 == 0 else nc.sync

@@ -51,7 +51,7 @@ def tile_attend_ghsort_tnh_pl_kernel(tc, wo, dyT, W, h, offs, out_0, out_1, out_
         ps = ctx.enter_context(tc.psum_pool(name="ps", bufs=1))
 
         def tile(name, shape, dtype, tag=None):
-            return sb.tile(shape, dtype, name=name, tag=tag or name, align_bytes=64)
+            return sb.tile(shape, dtype, name=name, tag=tag or name, align_bytes=256)
 
         def bank(k, shape):
             return ps.tile(shape, F32, name="bank", tag="bank%d" % k)
@@ -64,7 +64,7 @@ def tile_attend_ghsort_tnh_pl_kernel(tc, wo, dyT, W, h, offs, out_0, out_1, out_
         wo_raw = tile("wo_raw", [P, PACK, N], F32)
         h_cuts = (0, 640, 1280, PACK * N)
         h_part = [tile("h_part%d" % a, [P, h_cuts[a + 1] - h_cuts[a]], F32) for a in range(3)]
-        w_raw = shared.tile([P, PACK, N], F32, name="w_raw", offset=0, align_bytes=64)
+        w_raw = shared.tile([P, PACK, N], F32, name="w_raw", offset=0, align_bytes=256)
 
         h_rows = h.rearrange("(p j) c -> p (j c)", j=PACK)
         nc.sync.dma_start(out=dy_raw[:], in_=dyT.rearrange("(p j) c -> p j c", j=PACK))
@@ -214,11 +214,11 @@ def tile_attend_ghsort_tnh_pl_kernel(tc, wo, dyT, W, h, offs, out_0, out_1, out_
         cast_w(nc.vector.tensor_copy, 1, 0, wcut)
         quantise_dz(dz_first[:], 0, HALF)
         quantise(nc, w_codes[:, 0:HALF], w_scales[:, 0:HALF], w_bf[0][:], E4M3)
-        third = shared.tile([P, N], BF16, name="dz_third", offset=0, align_bytes=64)
+        third = shared.tile([P, N], BF16, name="dz_third", offset=0, align_bytes=256)
         dz_third = third[:]
         weave_dz(nc.scalar.copy, dz_third, 1, 0, P)
         quantise(nc, w_codes[:, HALF:N], w_scales[:, HALF:N], w_bf[1][:], E4M3)
-        last = shared.tile([P, N], BF16, name="dz_last", offset=1024, align_bytes=64)
+        last = shared.tile([P, N], BF16, name="dz_last", offset=1024, align_bytes=256)
         dz_last = last[:]
         weave_dz(nc.vector.tensor_copy, dz_last, 1, P, HALF)
         quantise_dz(dz_third, HALF, HALF + P)
@@ -229,7 +229,7 @@ def tile_attend_ghsort_tnh_pl_kernel(tc, wo, dyT, W, h, offs, out_0, out_1, out_
         y_codes = tile("y_codes", [P, N], U32)
         y_scales = tile("y_scales", [P, N], U8)
         y = [
-            shared.tile([P, PACK, HALF], F32, name="y0", offset=4096, align_bytes=64),
+            shared.tile([P, PACK, HALF], F32, name="y0", offset=4096, align_bytes=256),
             tile("y1", [P, PACK, HALF], F32),
         ]
         for a, (first, cuts) in enumerate(((4, (0, 1, 2, 3, 4)), (0, (0, 1, 2, 3, 4)))):

from contextlib import ExitStack

import concourse.mybir as mybir

F32 = mybir.dt.float32
BF16 = mybir.dt.bfloat16
I32 = mybir.dt.int32
U16 = mybir.dt.uint16
U32 = mybir.dt.uint32
U8 = mybir.dt.uint8
E4M3 = mybir.dt.float8_e4m3fn_x4
E5M2 = mybir.dt.float8_e5m2_x4
ALU = mybir.AluOpType
ACT = mybir.ActivationFunctionType

P = 128
PACK = 4
N = 512
HALF = N // 2
FLOPS = 2 * 2 * N * N * N


def quantise(nc, codes, scales, grouped, fmt):
    nc.vector.quantize_mx(out=codes.bitcast(fmt), scales=scales, in_=grouped)


def weave(copy, tile, planes, c0, c1):
    copy(
        out=tile[:, c0 * PACK : c1 * PACK].rearrange("p (c i j) -> p c j i", i=4, j=PACK),
        in_=planes[:, :, c0:c1].rearrange("p j (c i) -> p c j i", i=4),
    )


def product(nc, out, w_codes, w_scales, g_codes, g_scales):
    nc.tensor.matmul_mx(
        out=out,
        lhsT=w_codes.bitcast(E4M3),
        lhsT_scale=w_scales,
        rhs=g_codes.bitcast(E5M2),
        rhs_scale=g_scales,
        start=True,
        stop=True,
    )


def tile_attend_ghsort_tnh_pl_kernel(tc, wo, dyT, W, h, offs, out_0, out_1, out_2):
    nc = tc.nc
    with ExitStack() as ctx:
        sb = ctx.enter_context(tc.tile_pool(name="sb", bufs=1))
        shared = ctx.enter_context(tc.tile_pool(name="shared", bufs=1))
        ps = ctx.enter_context(tc.psum_pool(name="ps", bufs=1))

        def tile(name, shape, dtype, tag=None):
            return sb.tile(shape, dtype, name=name, tag=tag or name, align_bytes=256)

        def bank(k, shape):
            return ps.tile(shape, F32, name="bank", tag="bank%d" % k)

        def scalar_cast(out, in_):
            nc.scalar.activation(out=out, in_=in_, func=ACT.Copy)

        offsets = sb.tile([P, N // 16], U16, name="offsets")
        dy_raw = tile("dy_raw", [P, PACK, N], F32)
        wo_raw = tile("wo_raw", [P, PACK, N], F32)
        h_cuts = (0, 640, 1280, PACK * N)
        h_part = [tile("h_part%d" % a, [P, h_cuts[a + 1] - h_cuts[a]], F32) for a in range(3)]
        w_raw = shared.tile([P, PACK, N], F32, name="w_raw", offset=0, align_bytes=256)

        h_rows = h.rearrange("(p j) c -> p (j c)", j=PACK)
        nc.sync.dma_start(out=dy_raw[:], in_=dyT.rearrange("(p j) c -> p j c", j=PACK))
        nc.sync.dma_start(out=wo_raw[:], in_=wo.rearrange("(p j) c -> p j c", j=PACK))
        for a in range(3):
            nc.sync.dma_start(out=h_part[a][:], in_=h_rows[:, h_cuts[a] : h_cuts[a + 1]])
            if a == 1:
                nc.sync.dma_start(offsets[:], offs)
        nc.sync.dma_start(out=w_raw[:], in_=W.rearrange("(p j) c -> p j c", j=PACK))

        dy_bf = tile("dy_bf", [P, N * PACK], BF16)
        dy_codes = tile("dy_codes", [P, N], U32)
        dy_scales = tile("dy_scales", [P, N], U8)
        cut = 320
        weave(nc.vector.tensor_copy, dy_bf, dy_raw, 0, cut)
        weave(scalar_cast, dy_bf, dy_raw, cut, N)
        quantise(nc, dy_codes[:], dy_scales[:], dy_bf[:], E5M2)

        wo_bf = tile("wo_bf", [P, N * PACK], BF16)
        wo_cuts = (0, P, HALF, N)
        wo_codes = [tile("wo_codes%d" % a, [P, wo_cuts[a + 1] - wo_cuts[a]], U32) for a in range(3)]
        wo_plane = [wo_codes[0][:], wo_codes[1][:], wo_codes[2][:, 0:P], wo_codes[2][:, P:HALF]]
        wo_scales = tile("wo_scales", [P, N], U8)
        wo_dst = wo_bf[:].rearrange("p (t m j) -> p m j t", t=PACK, j=PACK)
        wo_src = wo_raw[:].rearrange("p j (m t) -> p m j t", t=PACK)

        def quantise_wo(a):
            c0, c1 = wo_cuts[a], wo_cuts[a + 1]
            quantise(nc, wo_codes[a][:], wo_scales[:, c0:c1], wo_bf[:, c0 * PACK : c1 * PACK], E4M3)

        mcut = 76
        nc.vector.tensor_copy(out=wo_dst[:, 0:mcut, :, 0:2], in_=wo_src[:, 0:mcut, :, 0:2])
        scalar_cast(wo_dst[:, mcut:P, :, 0:2], wo_src[:, mcut:P, :, 0:2])
        quantise_wo(0)
        quantise_wo(1)
        nc.vector.tensor_copy(out=wo_dst[:, :, :, 2:4], in_=wo_src[:, :, :, 2:4])

        slopes = tile("slopes", [P, PACK * N], F32)
        squares = {}

        def square(a):
            tag = ("squares0", "squares1", "wo_codes1")[a]
            squares[a] = tile("squares%d" % a, [P, h_cuts[a + 1] - h_cuts[a]], F32, tag=tag)
            nc.scalar.activation(out=squares[a][:], in_=h_part[a][:], func=ACT.Square)

        def affine_vector(a):
            nc.vector.tensor_scalar(
                out=slopes[:, h_cuts[a] : h_cuts[a + 1]], in0=squares[a][:], scalar1=-1.0, scalar2=1.0, op0=ALU.mult, op1=ALU.add
            )

        def affine_scalar(a, c0, c1):
            nc.scalar.activation(
                out=slopes[:, h_cuts[a] + c0 : h_cuts[a] + c1],
                in_=squares[a][:, c0:c1],
                func=ACT.Identity,
                scale=-1.0,
                bias=1.0,
            )

        dz_flat = tile("dz", [P, 7 * N], F32)

        def dz_half(a):
            span = 2 * N + 3 * HALF * a
            pairs = dz_flat[:, 0 : 2 * span].rearrange("p (a s) -> p a s", a=2)
            return pairs[:, :, 0 : 2 * N].rearrange("p a (b c) -> p a b c", b=2)[:, :, :, a * HALF : (a + 1) * HALF]

        def weave_dz(copy, dst, a, c0, c1):
            copy(
                out=dst.rearrange("p (c i a b) -> p c a b i", i=4, a=2, b=2),
                in_=dz_half(a)[:, :, :, c0:c1].rearrange("p a b (c i) -> p c a b i", i=4),
            )

        def fetch(t, c0, c1):
            first = t * N + (3 * HALF if t >= 2 and c0 >= HALF else 0)
            nc.vector.tensor_tensor(
                out=dz_flat[:, first + c0 : first + c1],
                in0=u[t][:].indirect(offsets[:, c0 // 16 : c1 // 16]),
                in1=slopes[:, t * N + c0 : t * N + c1],
                op=ALU.mult,
            )

        for a in range(2):
            square(a)
        affine_vector(0)
        quantise_wo(2)
        affine_vector(1)

        banks_u = [bank(t, [P, N]) for t in range(PACK)]
        for t in range(PACK):
            product(nc, banks_u[t][:], wo_plane[t], wo_scales[:, t * P : (t + 1) * P], dy_codes[:], dy_scales[:])

        u = [tile("u%d" % t, [P, 2 * N if t < 2 else N], F32) for t in range(PACK)]
        for t in range(2):
            nc.vector.memset(u[t][:, N : 2 * N], 0.0)
        for t in range(2):
            nc.scalar.copy(out=u[t][:, 0:N], in_=banks_u[t][:])
            fetch(t, 0, N)
        square(2)
        for t, pieces in ((2, (1,)), (3, ())):
            nc.scalar.copy(out=u[t][:], in_=banks_u[t][:])
            for k in pieces:
                affine_scalar(2, k * HALF, (k + 1) * HALF)
        negated = {}
        for t in range(2, PACK):
            negated[t] = tile("negated%d" % t, [P, HALF], F32)
            nc.scalar.activation(
                out=negated[t][:], in_=u[t][:].indirect(offsets[:, HALF // 16 : N // 16]), func=ACT.Copy, scale=-1.0
            )
        for t in range(2, PACK):
            fetch(t, 0, HALF)

        def finish(t):
            first = t * N + 4 * HALF
            k = 2 * (t - 2)
            nc.vector.scalar_tensor_tensor(
                out=dz_flat[:, first : first + HALF],
                in0=squares[2][:, k * HALF : (k + 1) * HALF],
                scalar=1.0,
                in1=negated[t][:],
                op0=ALU.subtract,
                op1=ALU.mult,
            )

        w_codes = tile("w_codes", [P, N], U32)
        w_scales = tile("w_scales", [P, N], U8)
        w_bf = [tile("w_bf%d" % a, [P, HALF * PACK], BF16) for a in range(2)]

        w_src = w_raw[:].rearrange("p j (m t) -> p m j t", t=PACK)

        def cast_w(cast, a, m0, m1):
            dst = w_bf[a][:].rearrange("p (t m j) -> p m j t", t=2, j=PACK)
            cast(out=dst[:, m0:m1], in_=w_src[:, m0:m1, :, 2 * a : 2 * a + 2])

        dz_codes = tile("dz_codes", [P, N], U32)
        dz_scales = tile("dz_scales", [P, N], U8)

        def quantise_dz(grouped, c0, c1):
            quantise(nc, dz_codes[:, c0:c1], dz_scales[:, c0:c1], grouped, E5M2)

        cast_w(scalar_cast, 0, 0, P)
        dz_first = tile("dz_first", [P, HALF * PACK], BF16)
        finish(2)
        weave_dz(nc.vector.tensor_copy, dz_first[:], 0, 0, HALF)
        finish(3)
        wcut = 56
        cast_w(scalar_cast, 1, wcut, P)
        cast_w(nc.vector.tensor_copy, 1, 0, wcut)
        quantise_dz(dz_first[:], 0, HALF)
        quantise(nc, w_codes[:, 0:HALF], w_scales[:, 0:HALF], w_bf[0][:], E4M3)
        third = shared.tile([P, N], BF16, name="dz_third", offset=0, align_bytes=256)
        dz_third = third[:]
        weave_dz(nc.scalar.copy, dz_third, 1, 0, P)
        quantise(nc, w_codes[:, HALF:N], w_scales[:, HALF:N], w_bf[1][:], E4M3)
        last = shared.tile([P, N], BF16, name="dz_last", offset=1024, align_bytes=256)
        dz_last = last[:]
        weave_dz(nc.vector.tensor_copy, dz_last, 1, P, HALF)
        quantise_dz(dz_third, HALF, HALF + P)
        quantise_dz(dz_last, HALF + P, N)

        y_rows = out_0.rearrange("(p t) c -> p t c", t=PACK)
        words = out_1.rearrange("g p c l -> (g p) (c l)").bitcast(I32)
        y_codes = tile("y_codes", [P, N], U32)
        y_scales = tile("y_scales", [P, N], U8)
        y = [
            shared.tile([P, PACK, HALF], F32, name="y0", offset=4096, align_bytes=256),
            tile("y1", [P, PACK, HALF], F32),
        ]
        for a, (first, cuts) in enumerate(((4, (0, 1, 2, 3, 4)), (0, (0, 1, 2, 3, 4)))):
            cols = slice(a * HALF, (a + 1) * HALF)
            for k, (t0, t1) in enumerate(zip(cuts, cuts[1:])):
                copy = nc.vector.tensor_copy if (a, t0) in ((0, 3), (1, 2)) else nc.scalar.copy
                planes = bank(first + k, [P, t1 - t0, HALF])
                for t in range(t0, t1):
                    m = slice(t * P, (t + 1) * P)
                    product(nc, planes[:, t - t0, :], w_codes[:, m], w_scales[:, m], dz_codes[:, cols], dz_scales[:, cols])
                copy(out=y[a][:, t0:t1, :], in_=planes[:])
                if a == 0 or t1 % 2 == 0:
                    t0 = t1 - 1 - a
                    nc.sync.dma_start(out=y_rows[:, t0:t1, cols], in_=y[a][:, t0:t1, :])
        y_bf = [tile("y_bf%d" % a, [P, PACK * HALF], BF16) for a in range(2)]

        def quantise_y(a, c0, c1):
            cols = slice(a * HALF + c0, a * HALF + c1)
            quantise(nc, y_codes[:, cols], y_scales[:, cols], y_bf[a][:, c0 * PACK : c1 * PACK], E4M3)

        for c0 in (0, P):
            weave(nc.vector.tensor_copy, y_bf[0], y[0], c0, c0 + P)
        quantise_y(0, 0, P)
        weave(nc.scalar.copy, y_bf[1], y[1], 0, P)
        weave(nc.vector.tensor_copy, y_bf[1], y[1], P, HALF)
        quantise_y(0, P, HALF)
        for c0 in (0, P):
            quantise_y(1, c0, c0 + P)
        nc.sync.dma_start(out=words, in_=y_codes[:].bitcast(I32))
        rows = out_2.rearrange("g q c -> (g q) c").bitcast(I32)
        for q in range(4):
            engine = nc.scalar if q % 2 == 0 else nc.sync
            engine.dma_start(out=rows[4 * q : 4 * q + 4, :], in_=y_scales[32 * q : 32 * q + 4, :].bitcast(I32))
